import numpy as np
CORES = [0,1,2,3,4,5,6,7,128,129,130,131,132,133,134,135,256,257,258,259,260,261,262,263,384,385,386,387,388,389,390,391]
N = 32
T = 128
ROUTE = [[[12,9,25,15],[23,25,20,22],[7,2,3,12],[31,19,22,27],[12,3,9,17],[13,7,27,15],[21,28,27,7],[4,3,28,1],[5,16,20,18],[7,19,31,10],[12,0,1,5],[13,16,11,14],[28,10,29,21],[17,5,3,21],[27,12,15,22],[25,21,5,29],[28,19,10,12],[9,3,25,10],[22,10,0,27],[26,25,18,27],[13,22,26,8],[2,13,1,28],[10,29,7,6],[14,15,13,20],[17,16,3,0],[22,27,20,28],[28,7,10,11],[19,23,20,27],[19,4,27,16],[16,26,6,2],[27,28,7,15],[17,10,1,9],[21,25,15,12],[2,17,12,18],[4,25,18,9],[8,28,12,22],[3,0,19,14],[28,9,13,24],[11,5,15,24],[1,18,19,4],[0,25,3,30],[27,2,28,31],[12,14,7,19],[10,0,8,27],[18,14,10,25],[29,4,31,19],[19,27,9,29],[27,3,16,30],[31,9,14,20],[30,13,31,1],[24,12,5,29],[30,7,22,12],[7,6,23,16],[16,25,26,21],[7,27,19,11],[16,15,22,13],[31,23,11,24],[26,24,5,6],[2,17,25,6],[3,19,27,31],[5,9,28,22],[1,14,25,19],[2,4,15,16],[21,31,6,15],[20,9,8,31],[13,22,10,3],[31,3,23,7],[25,16,2,1],[12,25,2,9],[31,24,28,18],[8,20,21,10],[22,19,3,10],[28,13,21,23],[11,17,26,28],[13,29,6,3],[2,22,4,14],[18,8,19,7],[8,9,14,26],[28,9,31,1],[19,24,11,14],[0,4,12,24],[20,6,14,17],[22,19,29,6],[0,6,26,8],[26,14,7,9],[16,4,15,19],[24,20,6,16],[9,26,10,28],[15,0,30,27],[9,1,18,23],[3,26,18,21],[30,16,1,29],[21,28,0,13],[24,11,6,25],[7,21,9,3],[31,26,17,1],[4,13,22,10],[22,28,29,31],[22,25,10,9],[3,18,25,31],[27,11,14,24],[24,27,16,0],[21,30,9,6],[11,14,2,0],[4,25,0,24],[25,1,19,20],[26,1,9,0],[0,8,25,27],[21,30,2,13],[3,14,29,21],[24,8,28,1],[13,28,22,12],[29,17,20,14],[2,8,30,20],[30,11,21,14],[12,3,20,27],[16,28,30,9],[24,17,31,7],[16,20,4,5],[25,8,11,7],[29,7,18,9],[21,9,20,11],[23,14,9,19],[19,10,9,18],[12,24,2,14],[29,3,23,31],[7,25,1,30],[10,26,1,20]],[[1,28,8,27],[9,19,0,12],[6,3,22,23],[10,25,24,16],[12,30,11,20],[1,2,30,31],[4,25,14,18],[8,5,11,25],[30,8,26,21],[13,15,25,16],[4,28,1,12],[9,16,14,19],[13,6,31,12],[12,21,31,23],[22,11,2,7],[16,2,3,14],[13,0,20,7],[15,9,6,4],[5,2,9,21],[4,23,17,13],[20,21,25,14],[21,15,10,17],[27,12,0,25],[21,23,29,22],[22,25,30,4],[28,10,20,17],[5,21,26,11],[21,16,0,17],[16,10,27,9],[23,6,11,15],[25,21,1,6],[20,15,2,11],[22,28,8,15],[15,12,0,18],[7,13,4,26],[24,25,1,5],[31,25,28,7],[27,26,14,23],[13,5,30,29],[30,17,8,29],[31,22,13,24],[20,17,5,4],[2,17,5,13],[4,25,12,1],[4,28,29,20],[5,9,14,26],[25,31,19,22],[5,31,30,27],[14,28,21,16],[23,6,9,4],[29,13,30,3],[26,11,1,18],[0,20,17,11],[1,25,30,14],[1,6,21,28],[24,17,15,14],[8,1,5,18],[17,13,11,31],[30,12,11,1],[18,11,2,17],[30,0,14,15],[6,27,30,12],[21,25,20,27],[8,27,31,18],[2,31,22,7],[4,0,13,22],[28,12,31,26],[18,4,28,12],[28,2,30,4],[3,1,5,30],[20,4,8,31],[24,11,6,18],[27,5,19,3],[1,20,17,26],[2,21,29,11],[0,1,17,20],[27,1,12,25],[6,17,30,24],[6,17,18,20],[24,14,2,26],[10,13,14,4],[18,3,0,14],[17,14,9,27],[31,3,5,13],[1,20,6,21],[15,16,28,6],[24,2,14,10],[31,9,18,27],[21,0,25,7],[25,28,20,21],[16,0,11,19],[14,16,7,3],[28,9,27,3],[26,4,30,31],[6,14,12,24],[11,3,26,31],[5,17,23,13],[25,18,26,7],[1,5,14,10],[27,13,1,21],[17,13,30,18],[15,4,11,16],[30,18,24,31],[31,8,29,19],[29,17,18,13],[25,26,12,0],[5,7,14,25],[28,31,0,10],[30,31,4,9],[13,1,31,20],[24,19,28,29],[18,20,28,22],[10,3,24,5],[0,15,7,18],[8,26,23,25],[0,8,29,31],[6,2,21,14],[24,12,15,29],[2,24,18,21],[14,18,16,24],[1,22,4,7],[26,11,29,31],[10,5,20,22],[5,26,29,22],[17,8,29,28],[21,30,28,18],[4,0,18,24],[26,9,22,3]],[[27,3,14,6],[10,25,6,2],[31,25,15,30],[28,22,17,0],[9,6,24,31],[0,26,9,21],[29,13,22,9],[8,31,6,11],[24,12,29,25],[0,4,16,25],[19,28,9,23],[10,28,1,3],[24,14,31,19],[18,4,27,10],[15,31,0,9],[2,21,20,27],[18,17,15,16],[19,14,29,23],[30,13,0,10],[11,29,5,21],[16,21,8,18],[15,18,6,19],[20,1,4,27],[5,31,11,1],[12,20,16,22],[12,30,2,4],[17,12,20,0],[16,9,30,4],[4,1,27,2],[21,1,4,17],[0,9,5,10],[17,26,5,30],[23,25,4,1],[17,24,18,6],[6,25,24,18],[22,15,9,29],[15,16,0,24],[3,16,18,14],[4,18,10,28],[17,24,23,7],[14,18,11,12],[9,19,5,21],[1,23,14,11],[5,2,17,8],[2,4,3,1],[23,13,12,20],[19,7,9,14],[21,24,26,1],[16,26,21,5],[1,3,13,26],[26,21,19,18],[22,20,19,27],[26,30,8,15],[20,0,26,7],[5,28,18,4],[5,13,31,9],[13,14,23,5],[30,28,12,11],[14,12,7,24],[12,1,11,23],[6,21,18,31],[19,6,8,11],[31,19,4,5],[9,31,0,2],[4,1,24,7],[13,27,26,15],[9,28,29,13],[21,25,3,5],[12,9,14,23],[13,27,23,14],[8,17,29,6],[31,26,30,2],[25,16,19,17],[18,26,10,25],[6,11,12,10],[27,20,23,24],[5,10,2,16],[25,1,13,12],[23,4,11,13],[15,2,11,1],[22,29,12,28],[4,29,10,22],[29,3,24,11],[30,14,29,17],[25,6,17,29],[23,11,3,16],[11,7,23,31],[2,18,19,15],[27,31,5,7],[28,29,24,19],[16,13,26,9],[29,13,6,2],[13,20,30,24],[23,9,5,4],[24,17,3,7],[23,26,30,13],[15,18,25,6],[7,21,18,23],[18,17,29,16],[13,19,2,14],[0,20,29,7],[27,7,1,17],[5,24,3,2],[31,25,12,14],[7,23,10,4],[21,4,13,23],[22,25,26,10],[27,7,20,9],[6,9,28,23],[25,24,0,17],[5,22,30,13],[24,5,20,30],[19,31,21,13],[1,11,27,19],[3,18,4,28],[31,25,21,4],[11,8,24,9],[12,1,6,5],[29,9,14,7],[18,15,1,9],[10,28,7,5],[7,28,9,3],[17,0,9,30],[31,1,14,20],[24,21,28,22],[24,9,20,29],[31,20,28,24],[8,18,15,21]],[[28,12,25,11],[21,22,0,13],[5,25,13,8],[26,8,12,4],[5,20,25,9],[16,9,7,6],[28,20,15,17],[26,11,16,17],[30,1,25,17],[25,1,2,12],[19,11,22,5],[17,30,12,15],[30,12,16,7],[10,30,27,12],[14,8,0,21],[19,15,23,20],[23,5,25,14],[4,1,28,16],[12,21,1,31],[19,6,22,4],[5,1,14,25],[18,6,25,11],[8,17,26,19],[19,26,24,30],[17,1,24,19],[6,30,29,5],[19,15,24,12],[12,0,18,31],[22,12,11,31],[24,10,14,1],[25,18,26,1],[16,23,31,12],[24,15,19,11],[17,30,12,4],[10,4,21,9],[15,6,2,12],[6,11,18,31],[23,15,16,28],[24,14,7,13],[7,1,11,18],[24,0,12,6],[29,11,21,24],[18,15,29,14],[30,22,27,9],[0,10,26,23],[11,10,29,21],[31,0,6,21],[8,13,30,4],[29,8,28,16],[5,0,9,21],[27,29,15,6],[16,17,30,9],[23,19,15,7],[31,30,24,1],[18,14,20,8],[25,26,8,7],[24,8,2,10],[25,2,17,7],[6,13,18,8],[6,2,30,0],[12,29,7,1],[9,6,13,19],[24,22,30,15],[5,30,18,19],[3,23,15,13],[11,25,16,7],[15,2,12,4],[9,29,4,11],[13,1,8,29],[2,5,0,23],[27,3,4,2],[3,16,1,28],[13,3,22,21],[0,14,3,2],[12,14,4,30],[15,7,13,29],[15,3,0,26],[26,20,15,1],[0,1,11,15],[26,24,2,1],[15,26,11,3],[16,30,3,6],[0,18,15,20],[2,26,28,5],[30,17,0,12],[6,20,24,30],[20,19,30,0],[2,14,5,4],[0,14,27,15],[17,24,2,1],[10,3,21,6],[14,22,25,16],[4,2,20,22],[13,16,4,8],[4,20,16,22],[8,26,14,4],[17,7,8,22],[7,19,17,12],[14,28,13,19],[24,17,11,7],[28,0,31,23],[1,29,27,10],[7,15,14,10],[1,25,4,23],[20,2,30,15],[7,0,19,10],[6,21,7,3],[20,21,15,0],[11,6,26,23],[10,30,13,24],[19,10,31,20],[9,27,1,29],[4,19,11,14],[13,4,14,24],[26,16,8,7],[20,18,31,10],[26,18,22,0],[12,5,19,8],[15,16,26,4],[15,7,27,5],[21,30,0,24],[3,15,21,25],[2,3,10,22],[20,15,26,6],[16,18,8,26],[4,19,22,11],[29,3,31,17],[14,23,10,24]],[[14,10,27,29],[2,12,7,8],[14,8,5,10],[12,2,5,27],[0,6,16,17],[11,4,19,23],[3,6,13,11],[8,5,29,31],[14,15,3,19],[26,8,17,24],[7,20,0,15],[4,21,31,7],[28,7,8,19],[2,5,22,12],[3,18,8,25],[30,25,5,23],[25,31,29,6],[25,1,8,30],[4,15,2,30],[18,31,23,29],[22,27,20,4],[1,6,19,2],[27,16,14,24],[31,18,30,29],[14,25,3,12],[0,20,31,19],[2,1,27,22],[14,8,3,9],[2,30,25,15],[4,15,3,28],[10,17,19,22],[3,7,29,16],[1,3,26,13],[8,16,4,29],[1,3,27,17],[4,5,12,9],[24,5,26,11],[8,12,10,13],[13,14,3,15],[21,24,29,5],[9,28,15,10],[14,13,10,21],[14,26,21,27],[27,10,6,19],[19,9,2,6],[28,15,27,7],[15,5,9,6],[27,11,31,6],[8,0,30,2],[12,2,20,3],[1,6,13,4],[19,20,31,11],[18,5,2,14],[25,30,24,22],[24,23,31,29],[7,12,17,21],[28,8,19,18],[0,11,10,18],[0,27,8,16],[30,9,10,2],[3,23,25,29],[22,17,21,5],[15,1,2,12],[18,5,25,31],[8,11,7,1],[2,4,26,3],[23,29,1,2],[17,14,0,19],[2,13,0,22],[1,6,20,28],[15,29,8,3],[30,3,18,0],[16,18,26,13],[10,5,17,0],[22,15,11,6],[31,13,8,21],[17,11,27,12],[31,17,15,26],[2,5,13,6],[3,26,25,5],[13,15,26,16],[1,6,18,9],[19,3,13,0],[10,8,15,29],[19,31,7,0],[16,12,9,20],[25,31,0,29],[25,31,22,11],[29,6,31,19],[28,19,10,17],[8,15,0,7],[28,16,11,23],[14,12,20,22],[28,5,7,10],[11,23,17,9],[21,0,18,6],[11,22,5,4],[8,13,29,15],[16,19,18,20],[8,17,12,6],[2,15,25,24],[9,24,30,3],[29,22,16,30],[5,0,24,29],[10,20,3,23],[27,10,29,11],[25,6,2,24],[3,19,0,25],[17,22,13,29],[25,3,1,6],[17,25,21,1],[13,26,9,27],[15,13,7,23],[17,7,19,3],[24,29,19,18],[12,0,20,29],[8,10,0,27],[10,18,3,7],[31,16,18,22],[5,17,31,8],[28,6,29,1],[25,14,3,6],[28,12,11,17],[27,23,28,10],[21,18,26,30],[5,30,23,8],[7,27,26,22],[17,9,4,24]],[[12,5,9,23],[15,19,12,4],[14,15,7,12],[6,17,22,26],[13,27,7,6],[31,3,27,29],[16,31,3,20],[30,19,9,29],[16,20,11,27],[8,29,25,30],[1,15,20,3],[21,25,13,27],[28,2,12,10],[31,1,5,17],[17,18,5,25],[8,18,29,20],[20,4,8,24],[8,0,13,22],[18,16,5,31],[11,24,21,5],[7,5,19,11],[0,1,13,10],[4,7,8,12],[16,12,21,22],[28,20,17,0],[29,18,8,9],[15,21,19,16],[27,4,13,10],[31,17,24,12],[3,29,21,23],[28,5,9,21],[27,10,3,16],[5,28,20,25],[6,15,17,19],[23,7,4,11],[23,15,4,3],[30,26,5,17],[28,24,23,13],[10,18,29,14],[27,20,3,13],[29,0,28,5],[24,3,15,2],[23,20,1,27],[14,26,22,20],[27,8,9,6],[25,2,16,8],[7,16,23,26],[19,14,30,21],[4,15,26,29],[9,17,23,1],[30,23,21,14],[19,12,6,28],[3,16,6,24],[13,23,21,30],[14,0,12,21],[11,17,18,14],[21,19,28,6],[7,23,1,0],[17,13,14,19],[30,7,6,5],[8,5,23,3],[17,6,2,5],[16,24,13,22],[8,28,22,23],[11,25,22,15],[24,11,20,3],[26,10,9,11],[16,14,30,8],[23,13,4,25],[5,4,16,7],[13,15,0,14],[23,18,20,17],[14,3,22,18],[31,8,25,1],[3,25,30,15],[10,11,15,31],[19,13,31,23],[30,27,29,22],[9,6,8,13],[5,30,25,10],[7,12,31,9],[13,7,31,1],[29,1,13,25],[25,13,0,18],[1,3,5,25],[13,20,29,10],[23,22,27,14],[13,17,20,11],[1,2,4,20],[27,3,13,5],[22,6,14,7],[14,28,10,6],[7,24,19,8],[26,8,27,16],[10,0,8,16],[18,29,4,6],[28,31,8,26],[27,22,3,23],[6,19,24,7],[29,10,18,28],[11,28,30,5],[25,9,17,11],[20,3,2,25],[23,18,15,27],[16,31,23,24],[28,25,22,12],[20,14,6,5],[14,4,16,0],[20,26,12,31],[16,12,25,30],[10,27,9,22],[17,12,4,20],[30,18,26,8],[5,25,7,15],[2,18,1,16],[24,5,12,0],[11,10,17,30],[28,5,10,1],[3,10,29,8],[21,3,27,8],[25,24,16,26],[15,19,20,25],[20,21,27,0],[29,17,27,26],[15,6,27,29],[10,21,25,3],[20,31,15,29],[14,28,13,23]],[[1,7,9,12],[25,31,23,1],[16,0,25,27],[0,30,4,7],[26,19,0,15],[10,30,31,23],[2,21,1,30],[11,22,30,12],[16,5,30,14],[28,18,20,0],[12,2,11,24],[31,26,12,13],[30,9,4,6],[24,14,3,17],[17,30,8,2],[2,25,9,0],[7,29,27,14],[31,4,29,10],[16,11,0,24],[8,1,12,19],[7,26,16,19],[25,29,11,3],[9,5,8,22],[0,2,10,29],[13,6,8,3],[1,17,22,31],[26,22,7,1],[3,30,24,15],[10,11,14,5],[29,3,7,20],[20,23,21,11],[31,1,9,13],[20,1,12,2],[12,15,1,24],[9,13,29,23],[13,14,16,6],[5,24,3,28],[16,25,28,22],[4,19,1,26],[31,27,12,19],[6,28,27,9],[20,26,28,1],[25,20,26,29],[19,13,1,31],[10,0,3,20],[27,19,18,4],[24,7,25,2],[11,10,15,25],[7,20,23,22],[11,14,28,5],[28,12,16,1],[30,29,7,0],[21,5,13,11],[19,16,18,24],[8,3,9,30],[18,16,24,21],[17,28,0,15],[22,31,26,17],[21,22,24,28],[3,7,15,25],[0,25,3,9],[15,31,19,22],[5,25,23,4],[18,31,7,10],[12,20,16,24],[10,2,24,30],[29,7,5,17],[19,7,21,27],[25,30,13,16],[2,24,28,27],[8,2,11,20],[25,12,6,11],[18,31,24,23],[1,21,3,24],[13,30,25,26],[2,24,12,1],[29,9,8,2],[23,3,21,6],[1,23,14,19],[13,6,24,26],[4,5,22,9],[3,6,15,7],[31,8,2,1],[8,16,19,14],[29,11,24,8],[8,22,24,20],[23,14,13,6],[0,4,12,18],[18,16,12,8],[8,24,9,11],[1,24,15,0],[31,11,0,17],[17,13,23,12],[0,8,19,21],[31,28,13,2],[22,12,28,7],[15,6,20,16],[23,22,15,6],[22,11,21,12],[25,2,18,14],[23,31,12,19],[1,11,10,14],[9,24,19,20],[0,18,6,31],[28,9,5,10],[31,7,13,0],[16,30,9,8],[18,21,9,25],[22,11,23,31],[12,11,18,26],[3,16,11,14],[10,17,24,0],[30,13,2,6],[10,11,17,1],[19,27,24,29],[23,11,4,28],[11,28,25,21],[3,27,4,8],[29,31,12,13],[15,30,17,2],[19,12,17,23],[14,5,6,1],[6,22,14,17],[10,31,17,13],[11,31,1,2],[2,25,20,18],[0,24,13,11],[8,7,29,24]],[[19,30,7,28],[3,10,23,0],[6,17,16,27],[18,2,30,16],[6,30,9,25],[26,14,30,4],[8,20,21,15],[7,20,17,18],[5,2,14,17],[13,5,3,18],[12,21,14,10],[17,28,24,27],[30,15,20,29],[16,2,26,19],[29,0,23,24],[13,7,6,20],[21,10,25,8],[26,20,31,12],[14,28,20,10],[23,10,5,15],[23,29,27,31],[19,14,3,16],[1,2,5,10],[21,10,11,23],[22,2,15,5],[22,9,25,3],[4,30,7,22],[28,7,24,23],[7,6,30,24],[2,28,4,23],[12,4,23,29],[29,1,6,3],[18,14,27,7],[15,3,2,19],[28,30,13,19],[18,17,16,28],[19,17,10,7],[4,27,3,22],[10,22,19,18],[17,12,15,18],[9,24,14,26],[2,22,31,26],[22,24,31,13],[16,17,19,24],[2,31,23,25],[15,23,28,0],[1,30,11,15],[21,1,5,16],[11,28,17,9],[27,4,13,24],[9,17,26,3],[12,30,18,8],[18,13,20,12],[26,4,17,31],[8,17,21,2],[27,23,18,16],[19,27,30,16],[8,21,19,13],[4,23,15,27],[24,5,22,11],[6,14,18,25],[24,15,5,7],[1,5,15,14],[11,1,18,22],[1,5,24,27],[31,10,19,16],[18,25,14,4],[31,11,9,23],[0,27,11,25],[6,16,9,2],[30,0,10,18],[15,16,26,30],[8,2,27,13],[21,9,12,4],[4,7,6,26],[22,9,3,11],[26,20,4,24],[11,0,27,7],[15,22,14,6],[23,9,16,15],[18,23,26,21],[16,12,28,14],[4,30,3,9],[8,7,31,10],[9,17,1,31],[19,3,31,8],[24,7,9,19],[8,25,5,29],[31,5,30,18],[3,25,4,17],[7,21,6,20],[17,15,25,4],[7,14,30,5],[23,24,9,1],[27,7,3,24],[31,25,28,4],[21,9,0,3],[13,23,25,16],[18,12,20,5],[17,15,29,23],[8,29,15,17],[20,31,14,25],[21,11,22,23],[7,16,15,5],[22,16,8,27],[27,21,24,19],[2,28,6,16],[5,21,0,3],[4,3,11,28],[27,30,29,6],[2,12,9,11],[22,9,25,6],[2,6,9,5],[21,16,7,27],[6,16,11,8],[27,6,10,11],[6,3,9,1],[1,27,16,20],[21,13,10,23],[10,5,14,12],[1,26,5,14],[23,13,25,29],[16,28,29,18],[15,28,6,19],[14,2,28,15],[30,3,12,29],[13,9,29,3],[18,27,1,2]],[[20,7,19,25],[28,12,9,10],[26,9,6,12],[31,0,18,1],[1,27,20,23],[29,16,28,15],[17,16,3,27],[5,16,27,26],[15,12,9,4],[22,15,2,1],[5,6,29,13],[22,20,10,27],[30,4,14,17],[19,23,24,7],[1,15,22,9],[31,15,27,14],[3,24,29,27],[29,7,28,24],[21,26,29,5],[16,8,28,17],[31,22,24,10],[26,6,24,29],[4,27,26,8],[5,24,21,7],[28,10,31,5],[30,28,19,25],[4,28,20,12],[3,8,1,28],[29,31,8,26],[3,23,0,10],[20,8,27,15],[29,1,12,15],[30,20,4,27],[4,22,10,9],[9,25,7,26],[30,16,29,19],[4,8,12,11],[25,14,30,4],[23,25,28,0],[4,15,5,17],[26,14,22,21],[20,13,11,10],[25,20,14,10],[6,23,12,18],[9,17,26,0],[6,1,4,26],[20,22,5,28],[3,4,18,31],[0,16,11,29],[26,29,19,9],[20,31,23,8],[5,13,11,1],[27,7,17,28],[20,17,22,12],[0,29,3,2],[6,14,19,17],[0,6,20,22],[26,12,3,14],[23,11,31,20],[19,25,1,8],[17,7,25,28],[4,8,28,27],[18,22,15,27],[8,12,25,28],[1,12,23,5],[14,16,7,26],[9,25,0,21],[24,17,25,12],[1,13,0,12],[10,31,16,21],[25,6,23,16],[25,7,9,21],[9,12,20,4],[31,23,3,18],[9,22,19,8],[20,10,14,15],[15,28,31,9],[3,30,1,19],[21,31,26,5],[31,9,12,0],[31,18,30,0],[6,19,21,9],[22,10,9,7],[24,13,17,10],[3,5,13,10],[31,8,13,26],[21,23,13,19],[25,13,15,9],[30,5,3,20],[20,26,28,24],[28,9,16,27],[7,3,17,10],[22,19,24,6],[24,29,1,17],[1,3,29,4],[19,20,10,12],[24,30,18,7],[1,16,7,26],[4,3,7,23],[14,16,5,22],[7,30,3,1],[27,7,2,11],[1,2,20,18],[10,30,19,8],[25,15,26,18],[0,11,10,16],[16,17,11,4],[22,19,8,29],[29,31,22,20],[1,25,20,22],[13,30,18,10],[13,7,22,28],[24,3,5,26],[5,18,31,25],[24,0,2,12],[11,2,27,17],[3,2,23,22],[28,5,20,7],[21,10,9,8],[23,9,6,29],[18,20,31,3],[30,21,0,24],[9,25,18,14],[25,1,11,29],[11,28,31,2],[17,24,2,13],[16,24,30,20],[5,6,24,1]],[[24,31,15,13],[15,11,3,24],[27,29,16,9],[16,20,14,22],[5,22,1,20],[23,2,4,31],[13,31,18,12],[9,27,30,2],[0,12,30,5],[16,25,30,1],[31,29,12,20],[9,1,23,2],[19,13,17,7],[12,21,11,8],[22,25,29,18],[22,30,6,2],[0,27,14,8],[21,25,14,18],[28,16,17,26],[27,23,31,22],[19,14,5,29],[12,14,22,25],[13,6,7,0],[16,0,17,26],[26,20,22,15],[13,23,15,31],[16,28,14,5],[7,14,3,12],[10,26,11,5],[16,4,20,3],[6,1,13,20],[24,12,16,13],[3,4,13,8],[19,18,29,15],[26,4,20,0],[20,28,24,6],[9,18,11,22],[24,12,0,18],[12,25,23,15],[29,4,10,0],[25,16,15,17],[0,25,18,16],[24,29,31,17],[7,14,25,26],[31,29,24,22],[31,6,25,8],[14,22,23,21],[1,8,5,26],[6,28,2,30],[7,9,11,18],[4,21,18,23],[8,1,20,10],[2,22,7,3],[22,12,13,29],[27,30,22,15],[30,4,11,2],[2,15,1,17],[7,11,18,2],[21,14,18,3],[7,27,23,25],[22,14,21,1],[23,4,11,16],[26,6,2,1],[5,29,14,27],[29,8,23,9],[30,14,1,15],[7,15,20,9],[0,4,27,14],[28,21,25,11],[14,9,29,17],[3,14,0,5],[24,6,20,2],[18,8,28,0],[6,11,20,7],[21,18,31,0],[18,1,12,11],[9,31,24,3],[18,8,9,22],[20,30,21,18],[9,20,0,1],[2,4,17,11],[28,19,24,4],[0,4,16,20],[12,9,31,28],[23,1,30,18],[12,13,4,6],[22,15,19,2],[4,8,23,30],[27,7,30,25],[0,12,16,14],[20,27,31,23],[18,16,6,11],[7,4,3,17],[15,12,20,1],[17,22,12,4],[25,23,29,14],[19,17,5,26],[27,1,29,16],[16,3,15,5],[2,7,28,3],[12,8,7,9],[20,30,2,18],[25,11,14,1],[6,0,20,4],[13,29,9,15],[30,6,1,17],[1,26,4,15],[6,28,13,15],[24,25,2,15],[15,10,30,12],[2,18,4,23],[17,31,16,9],[8,28,17,14],[6,5,2,25],[1,13,25,9],[31,4,22,17],[20,22,29,25],[4,11,6,31],[9,3,14,12],[27,19,20,29],[8,11,0,31],[23,4,24,15],[3,25,18,15],[7,17,9,8],[11,2,18,16],[3,6,1,15],[5,16,13,26],[23,28,5,9]],[[19,2,25,28],[11,18,0,9],[25,8,27,5],[12,28,19,1],[30,12,19,22],[13,14,28,5],[8,30,19,0],[19,4,30,15],[25,12,23,29],[8,1,6,20],[4,21,28,1],[25,6,31,0],[19,24,22,13],[18,15,6,25],[16,9,0,30],[26,22,28,15],[10,29,26,28],[20,15,16,21],[16,30,29,12],[22,2,29,19],[28,29,30,15],[19,23,29,7],[20,14,28,4],[16,4,22,28],[1,12,9,31],[12,5,0,27],[20,18,11,30],[30,16,22,31],[18,3,30,24],[31,27,23,11],[23,3,7,28],[26,17,24,19],[6,22,1,26],[31,5,1,17],[21,29,27,12],[2,27,30,7],[13,28,27,25],[2,0,28,21],[7,9,14,29],[27,10,12,23],[2,17,16,3],[1,28,15,13],[19,30,7,14],[15,1,4,3],[9,8,13,14],[11,23,29,0],[15,22,19,20],[20,14,22,27],[0,6,31,3],[1,4,27,7],[5,22,0,23],[15,21,7,3],[1,12,15,18],[14,27,0,22],[15,6,19,16],[19,29,10,12],[24,20,5,23],[27,28,11,26],[11,27,8,26],[0,2,3,26],[5,22,17,29],[17,30,2,9],[27,2,26,28],[4,6,11,9],[0,28,20,15],[4,27,14,13],[28,12,18,31],[21,1,10,28],[18,27,29,5],[3,31,30,17],[24,17,30,0],[26,30,18,13],[9,20,1,0],[20,0,12,23],[5,21,28,16],[0,22,15,18],[10,0,2,23],[5,23,10,3],[20,12,8,10],[26,9,24,5],[1,11,4,15],[31,0,7,3],[14,15,0,3],[18,17,30,12],[30,29,17,25],[10,22,16,14],[30,22,29,3],[26,24,17,21],[12,5,14,13],[6,15,20,8],[13,12,16,29],[19,7,15,0],[9,8,0,5],[23,10,8,1],[24,8,0,22],[28,6,2,29],[19,12,29,7],[20,1,28,10],[0,12,25,14],[4,3,1,0],[8,5,16,0],[31,23,25,22],[18,29,15,13],[19,9,1,16],[6,0,31,11],[20,12,4,2],[4,30,12,31],[23,29,21,2],[28,4,16,5],[23,6,24,25],[2,10,24,16],[30,20,22,14],[20,25,4,24],[1,6,10,17],[25,31,9,22],[14,18,25,2],[12,16,11,25],[19,28,1,10],[21,1,23,15],[12,14,5,30],[14,2,6,16],[7,31,23,10],[7,12,6,15],[17,29,26,5],[12,1,10,17],[12,30,25,9],[4,15,24,6],[10,14,24,16]],[[13,26,3,21],[24,11,20,28],[0,16,25,27],[7,0,27,16],[2,21,29,6],[1,17,20,3],[17,21,15,6],[4,29,12,10],[3,31,4,29],[14,18,23,31],[18,6,22,15],[24,27,23,20],[4,24,10,16],[17,31,25,1],[10,3,18,2],[30,23,14,16],[9,0,23,12],[1,25,21,31],[15,29,13,31],[15,2,29,12],[13,23,9,21],[14,28,31,5],[25,27,23,18],[13,11,9,27],[3,28,19,30],[23,21,11,31],[28,9,26,4],[9,30,7,6],[8,16,12,14],[20,11,24,27],[2,16,26,17],[3,12,25,5],[21,25,19,16],[19,15,7,0],[19,26,9,29],[14,4,20,24],[20,7,5,21],[2,19,4,17],[7,12,25,28],[2,12,17,10],[27,8,16,25],[17,12,24,1],[10,24,25,9],[11,1,30,12],[5,8,28,15],[18,1,20,15],[19,11,14,21],[7,18,15,0],[29,28,6,20],[19,30,7,24],[22,5,26,14],[12,15,7,18],[24,2,20,30],[23,5,0,26],[10,19,7,24],[12,27,25,14],[1,5,9,29],[0,5,25,31],[5,19,23,26],[3,13,21,0],[25,17,3,4],[22,23,16,6],[5,10,9,27],[23,31,28,1],[14,5,12,7],[31,12,17,7],[0,29,6,4],[14,30,21,26],[12,27,18,11],[17,30,7,16],[21,24,27,5],[12,6,31,26],[27,26,24,7],[24,30,6,10],[5,24,4,12],[14,12,23,18],[13,21,22,29],[27,11,17,14],[19,7,31,27],[21,5,13,19],[27,20,14,11],[4,7,22,11],[12,19,22,15],[22,7,20,26],[8,6,20,15],[17,10,2,14],[0,24,1,4],[26,22,23,16],[25,5,2,16],[26,23,21,27],[8,30,14,15],[20,5,13,8],[10,14,11,16],[11,27,21,5],[5,31,8,15],[13,4,16,22],[18,26,3,31],[17,25,3,13],[9,2,15,23],[1,19,14,27],[2,27,28,20],[6,5,0,16],[25,5,13,12],[14,21,24,17],[16,13,7,27],[17,28,9,31],[18,23,25,31],[12,21,23,7],[6,22,11,13],[20,14,3,12],[6,12,26,29],[4,11,9,17],[5,11,27,26],[1,10,31,24],[12,29,25,30],[16,31,22,30],[28,19,8,1],[22,0,18,23],[6,16,28,8],[30,17,20,10],[21,1,30,18],[19,24,4,0],[23,22,21,11],[20,19,10,2],[11,20,27,7],[5,21,11,20],[3,9,5,29],[17,1,7,6]],[[1,28,29,14],[4,2,15,10],[24,1,13,7],[7,15,9,12],[3,2,1,17],[20,13,28,2],[31,18,4,9],[7,8,2,16],[23,26,12,25],[19,14,3,1],[3,16,1,28],[21,19,27,15],[19,10,23,30],[0,28,5,11],[7,21,22,3],[29,10,21,12],[10,23,12,30],[24,3,23,10],[14,21,24,29],[12,9,20,22],[15,16,31,21],[26,16,5,18],[22,10,17,16],[9,11,19,17],[4,9,3,16],[10,12,13,25],[30,22,11,13],[18,16,11,30],[6,21,0,24],[6,10,19,24],[5,18,11,12],[4,29,3,18],[31,11,22,13],[18,25,26,4],[26,24,4,10],[8,27,21,24],[15,10,4,7],[17,3,21,12],[23,3,12,15],[1,6,30,12],[2,8,11,19],[19,20,4,8],[20,17,13,10],[17,25,15,8],[6,0,3,29],[5,11,23,25],[20,1,23,29],[27,4,8,19],[24,15,23,16],[4,22,7,31],[11,9,18,0],[10,24,3,23],[6,23,24,4],[24,30,9,17],[15,18,6,20],[26,17,13,21],[2,30,0,21],[20,12,24,4],[6,10,26,3],[29,26,16,27],[2,31,27,26],[20,17,22,6],[21,4,11,19],[6,27,18,23],[2,29,19,25],[14,19,23,15],[28,9,0,21],[19,21,22,20],[13,0,17,6],[17,10,30,25],[17,0,26,1],[0,25,23,1],[12,2,28,31],[22,28,18,2],[6,16,4,18],[14,25,31,10],[14,16,10,12],[28,9,19,1],[23,13,4,19],[14,18,28,27],[19,18,26,25],[18,29,23,14],[31,3,11,26],[5,27,26,30],[17,9,0,21],[22,26,4,25],[30,4,3,16],[27,28,21,20],[9,1,10,20],[1,3,9,30],[30,10,25,18],[23,16,4,14],[1,31,26,27],[5,6,30,11],[20,14,5,23],[14,8,26,20],[14,22,0,6],[7,18,14,21],[7,31,2,25],[30,6,7,27],[18,2,22,25],[2,13,12,18],[9,28,30,15],[31,24,19,22],[6,23,29,27],[17,11,8,14],[27,8,10,20],[19,9,10,20],[17,9,22,4],[25,11,29,18],[17,8,0,23],[6,4,21,7],[19,15,27,14],[15,0,10,27],[22,31,9,25],[31,11,9,4],[19,20,2,7],[14,22,19,28],[12,10,25,16],[2,26,20,4],[22,24,28,9],[20,19,13,31],[31,8,23,18],[26,9,5,16],[3,2,4,28],[25,15,4,24],[25,3,18,20],[21,19,4,22]],[[7,0,17,2],[6,16,29,19],[15,14,19,28],[6,5,2,11],[14,31,17,8],[12,7,6,20],[31,26,8,29],[25,20,10,6],[8,22,12,3],[27,3,25,17],[31,30,24,13],[30,22,15,24],[28,23,16,5],[12,11,24,19],[25,31,17,15],[9,26,22,11],[4,25,18,2],[25,4,1,14],[23,1,17,29],[21,9,10,0],[2,27,0,20],[22,31,5,11],[1,0,12,23],[19,24,22,25],[22,30,8,15],[7,22,21,18],[16,20,9,12],[1,30,22,31],[23,24,19,12],[6,20,7,27],[10,2,29,16],[12,8,15,28],[3,15,6,25],[14,11,30,23],[6,25,24,26],[30,16,12,24],[8,23,21,2],[9,14,23,24],[9,4,2,0],[10,31,4,15],[19,29,5,22],[16,3,2,23],[14,29,6,28],[22,15,24,10],[23,24,25,8],[7,28,24,26],[3,19,12,22],[5,6,2,10],[8,15,16,9],[7,17,22,31],[1,20,9,28],[12,8,14,1],[18,23,19,25],[31,18,27,15],[30,17,16,11],[7,5,16,14],[27,29,31,23],[19,12,6,2],[11,2,27,24],[4,31,18,28],[12,22,31,8],[9,6,10,3],[11,28,26,24],[17,13,27,23],[10,29,5,20],[15,14,17,8],[15,8,27,23],[0,25,17,13],[26,25,12,13],[21,30,28,13],[11,30,19,5],[15,21,5,22],[8,6,29,2],[7,30,21,29],[18,13,14,3],[19,28,0,22],[8,9,16,7],[6,20,5,0],[16,26,10,29],[14,12,19,7],[16,9,13,17],[27,31,7,3],[9,23,15,5],[29,16,21,1],[11,18,2,14],[31,6,18,28],[16,26,11,18],[16,1,28,24],[26,18,11,12],[13,8,5,18],[21,10,24,8],[1,3,23,20],[30,28,8,25],[22,31,3,20],[24,6,12,8],[19,29,4,11],[20,1,13,27],[13,7,6,24],[12,28,11,6],[25,15,6,27],[13,11,29,9],[11,1,23,16],[25,28,22,3],[12,2,5,9],[15,21,1,12],[13,24,5,6],[11,30,13,9],[11,30,27,31],[19,13,4,15],[18,5,4,15],[9,31,22,14],[10,25,8,23],[0,5,15,3],[11,12,27,25],[0,12,2,22],[5,25,23,3],[2,18,5,16],[11,12,6,28],[29,20,5,16],[31,17,10,22],[29,13,15,27],[13,3,28,7],[12,13,7,10],[9,20,6,10],[26,6,14,29],[12,11,17,28],[26,19,7,6],[21,29,30,23]],[[25,5,1,30],[25,18,27,26],[9,12,16,8],[13,8,22,30],[2,1,20,18],[31,26,16,27],[9,28,10,30],[23,27,30,14],[9,16,5,27],[9,22,15,21],[30,17,31,4],[29,25,1,17],[10,13,1,11],[15,16,9,13],[0,2,27,24],[3,31,26,24],[18,16,31,20],[2,18,20,10],[8,9,4,6],[29,7,4,8],[7,16,2,6],[3,30,14,25],[2,15,6,17],[3,16,0,8],[10,30,2,6],[27,24,26,25],[20,31,8,2],[16,12,2,17],[6,12,16,20],[4,20,7,11],[4,25,12,19],[31,26,1,21],[30,25,13,3],[6,16,24,11],[19,31,24,2],[19,26,28,13],[18,23,15,11],[18,31,6,14],[12,11,29,28],[1,7,11,4],[8,4,25,22],[24,16,3,28],[10,9,13,22],[14,3,20,31],[27,8,9,25],[16,6,9,8],[18,20,13,12],[10,0,3,12],[24,11,25,12],[17,23,4,9],[25,29,20,7],[0,4,12,5],[7,26,12,1],[15,11,30,14],[3,25,18,31],[29,1,20,8],[29,31,11,16],[19,2,21,29],[29,2,21,6],[0,27,12,26],[20,4,25,13],[15,1,29,20],[25,26,31,12],[1,23,4,22],[7,26,6,0],[3,27,26,13],[11,0,19,24],[10,3,4,26],[30,11,3,9],[9,10,30,14],[3,22,28,11],[23,24,3,22],[12,30,1,26],[30,23,20,7],[5,17,0,25],[26,12,19,7],[5,12,14,16],[21,15,0,28],[31,21,15,20],[21,30,6,10],[20,11,30,13],[18,2,28,12],[4,23,18,15],[8,12,16,17],[22,16,9,18],[5,20,27,13],[17,3,16,6],[6,2,11,17],[18,15,24,19],[8,13,16,3],[21,0,22,8],[19,24,12,15],[14,27,22,25],[15,17,25,8],[27,18,23,31],[23,1,14,18],[29,11,13,31],[11,3,10,20],[18,25,16,22],[31,28,23,9],[22,12,15,21],[11,9,15,5],[13,2,4,27],[17,13,29,14],[27,18,20,2],[28,27,14,24],[12,7,23,10],[1,31,17,23],[2,0,16,31],[9,20,1,3],[17,12,7,11],[12,2,6,20],[31,5,30,4],[3,4,8,7],[26,3,28,12],[1,16,8,4],[24,23,30,4],[27,8,13,30],[0,28,26,31],[21,31,27,28],[26,0,24,15],[21,10,2,30],[14,27,9,16],[30,1,20,25],[16,2,0,25],[17,28,14,20],[28,16,15,7],[30,17,9,14]],[[30,20,21,5],[17,1,9,16],[18,9,4,1],[29,31,14,11],[9,5,17,30],[0,23,28,14],[0,5,23,26],[12,0,28,6],[1,6,12,9],[10,23,15,20],[14,5,18,2],[17,21,6,24],[9,1,23,10],[21,16,23,25],[23,1,14,9],[14,22,9,27],[26,7,14,9],[22,10,1,16],[16,0,4,15],[13,31,16,9],[20,30,12,18],[27,14,25,31],[8,27,28,3],[18,23,25,24],[23,17,0,27],[24,11,10,8],[18,3,10,13],[30,6,20,27],[5,9,18,11],[27,20,21,29],[15,3,8,25],[21,11,20,22],[7,12,9,21],[19,4,12,5],[9,22,12,27],[12,18,3,5],[6,3,22,26],[22,15,2,1],[29,23,3,11],[12,20,26,22],[17,11,19,23],[13,17,7,8],[19,31,17,30],[0,30,27,21],[22,23,31,21],[20,29,15,28],[15,21,22,9],[12,16,24,1],[3,4,27,22],[2,11,16,28],[28,8,5,21],[16,29,5,26],[25,23,13,16],[0,1,17,10],[24,23,0,14],[22,18,6,19],[9,20,17,14],[24,30,29,19],[2,27,13,16],[16,21,31,23],[29,15,2,28],[5,8,20,18],[10,14,8,26],[14,17,1,18],[22,20,15,25],[15,24,21,8],[5,12,17,24],[3,22,1,7],[15,6,25,16],[14,5,27,0],[26,31,9,18],[17,3,8,28],[14,11,22,23],[29,21,2,14],[26,16,1,13],[8,29,26,16],[12,11,30,18],[24,7,20,12],[29,31,24,6],[5,10,3,14],[22,30,7,2],[22,11,17,23],[7,21,30,25],[1,23,11,27],[13,16,22,8],[19,5,27,8],[14,8,7,26],[9,1,15,3],[27,30,8,1],[30,21,17,15],[25,22,31,12],[0,18,28,24],[23,6,29,1],[9,4,6,16],[6,31,11,10],[9,3,8,25],[3,14,8,7],[31,24,29,30],[26,24,22,15],[28,26,21,4],[29,28,18,27],[15,6,12,18],[5,29,30,20],[30,22,18,24],[23,1,12,24],[30,23,4,28],[3,13,25,5],[9,30,20,21],[12,10,16,29],[5,20,18,21],[9,15,24,6],[18,26,13,10],[29,14,30,0],[14,13,29,2],[20,11,17,2],[27,24,30,5],[8,26,21,27],[0,3,12,8],[11,0,26,9],[30,22,25,16],[8,24,30,23],[14,9,17,8],[21,0,9,16],[19,22,27,25],[14,5,3,4],[22,27,31,17],[31,19,14,30],[21,0,1,27]],[[16,19,10,27],[27,29,25,7],[6,25,20,11],[20,0,11,31],[27,26,29,13],[11,18,1,30],[12,8,13,26],[28,13,6,15],[30,31,24,4],[6,11,23,28],[5,28,11,30],[28,9,20,18],[5,27,23,30],[6,15,14,23],[20,25,0,26],[21,22,24,12],[26,0,29,20],[30,31,3,24],[16,10,1,18],[30,15,8,31],[10,11,1,27],[19,26,7,0],[25,17,3,27],[25,31,4,13],[19,18,4,7],[2,5,7,1],[5,0,17,29],[24,30,13,12],[3,28,25,22],[13,12,8,9],[25,5,11,13],[10,16,25,9],[15,3,9,24],[8,20,4,3],[25,3,10,19],[29,13,20,8],[1,16,18,21],[14,0,10,17],[7,8,10,12],[30,23,7,19],[23,18,11,2],[12,14,11,22],[8,27,5,12],[18,27,3,1],[12,4,16,29],[17,30,5,12],[28,31,16,9],[26,4,14,11],[6,10,15,31],[9,24,28,12],[25,10,13,22],[30,18,22,20],[26,7,4,22],[30,13,6,8],[26,30,4,9],[20,29,26,24],[3,21,27,13],[28,30,20,12],[19,22,6,3],[12,31,24,1],[28,23,29,19],[24,8,13,16],[24,31,6,4],[26,10,22,30],[13,8,19,10],[18,21,1,12],[27,20,3,23],[25,14,27,13],[0,22,14,16],[12,14,5,15],[11,7,10,28],[9,14,23,27],[7,3,22,11],[24,17,6,27],[22,9,13,18],[7,20,29,14],[24,22,15,6],[22,20,29,12],[14,9,16,31],[8,25,23,30],[2,20,26,12],[5,31,1,29],[30,2,19,15],[15,2,29,3],[4,12,25,8],[18,17,8,14],[13,12,5,1],[20,7,17,19],[9,7,5,21],[19,20,30,4],[9,21,23,6],[19,11,29,13],[14,5,6,25],[13,15,3,22],[14,18,19,10],[11,9,25,6],[25,14,24,10],[6,22,21,26],[29,30,15,21],[7,23,27,16],[4,9,14,23],[1,30,4,2],[17,1,10,9],[6,20,9,26],[10,19,31,14],[15,3,23,2],[29,15,7,18],[4,11,12,30],[31,6,14,17],[30,15,14,22],[24,2,10,14],[30,15,28,12],[23,17,21,11],[29,3,5,6],[26,28,0,16],[10,4,12,5],[10,25,23,0],[9,17,25,5],[25,20,11,8],[20,25,18,7],[12,15,2,1],[10,7,8,26],[29,26,5,3],[29,9,11,23],[10,30,15,7],[10,24,27,9],[15,24,27,14],[15,27,5,19]],[[4,11,8,13],[31,19,8,2],[8,28,30,31],[25,1,16,14],[16,3,31,0],[6,28,19,7],[6,16,22,20],[15,1,13,28],[17,10,0,14],[15,28,2,5],[27,25,8,16],[31,30,18,17],[26,27,24,1],[1,30,29,12],[14,25,4,17],[3,1,30,11],[5,18,0,2],[0,27,11,7],[26,9,20,18],[7,25,20,16],[2,26,13,19],[19,6,0,27],[13,27,12,4],[22,19,25,1],[2,23,5,13],[7,23,11,9],[30,8,19,20],[14,28,20,10],[11,28,30,1],[14,27,24,30],[12,28,1,30],[16,28,19,25],[17,23,5,27],[26,10,21,9],[18,20,13,15],[14,15,27,1],[18,4,7,26],[13,3,8,17],[22,17,15,4],[23,0,20,27],[26,10,3,7],[3,31,26,11],[18,14,27,25],[11,14,12,9],[14,25,15,29],[2,0,16,19],[3,0,7,2],[18,25,13,14],[22,9,14,5],[25,19,14,30],[20,19,10,3],[25,27,28,5],[24,2,5,15],[30,21,26,5],[8,12,17,3],[5,13,20,0],[26,12,19,10],[25,11,20,8],[9,22,1,4],[22,18,19,6],[24,30,7,10],[7,21,27,24],[31,0,8,21],[19,8,7,22],[12,31,18,24],[28,0,31,10],[1,12,19,2],[7,13,0,1],[23,13,12,6],[14,5,20,1],[9,1,2,7],[7,26,31,15],[6,23,27,4],[15,13,28,12],[16,17,29,20],[1,29,30,19],[16,31,26,6],[23,7,4,15],[4,1,0,27],[22,2,24,28],[6,15,21,4],[1,8,29,0],[23,10,12,30],[11,2,25,30],[21,30,25,9],[10,12,25,6],[24,29,21,13],[17,7,15,20],[9,19,6,24],[3,7,14,6],[20,2,14,1],[26,23,29,17],[8,1,25,3],[25,0,18,6],[1,15,2,19],[23,10,8,22],[0,11,24,22],[26,0,23,2],[27,16,26,1],[1,7,31,3],[8,30,3,0],[27,0,26,16],[5,6,11,18],[3,0,1,20],[23,1,17,24],[8,27,12,28],[28,11,7,12],[14,2,26,3],[5,14,0,24],[13,8,3,5],[5,30,25,3],[4,23,30,12],[28,1,23,31],[26,20,6,9],[24,27,23,8],[13,30,25,21],[2,9,5,17],[11,28,7,4],[23,6,27,17],[9,8,0,2],[18,26,28,23],[21,13,14,10],[24,30,3,18],[9,1,28,21],[18,1,10,0],[25,5,11,6],[16,29,31,9],[16,23,26,22]],[[11,2,24,16],[29,2,7,5],[15,20,1,7],[10,1,18,15],[19,23,27,24],[5,29,7,2],[29,3,2,4],[26,30,2,7],[31,3,24,23],[5,6,2,30],[5,13,18,12],[14,19,25,23],[14,29,24,22],[23,3,31,19],[31,2,21,16],[7,6,5,28],[16,18,20,28],[22,24,20,11],[18,10,25,1],[8,17,24,25],[23,22,13,14],[21,19,28,27],[26,19,0,16],[6,26,21,13],[1,28,14,11],[20,2,12,10],[10,3,27,31],[20,23,1,5],[13,10,21,4],[24,10,31,30],[21,6,20,27],[31,29,19,9],[10,28,3,22],[27,15,28,23],[19,29,10,25],[31,5,28,29],[30,31,22,21],[17,5,24,2],[21,24,11,10],[11,30,21,29],[11,10,13,28],[10,31,22,30],[16,3,17,11],[6,15,18,27],[20,29,22,2],[28,8,4,14],[27,13,9,0],[5,16,26,9],[3,20,2,13],[25,4,21,17],[17,23,26,29],[30,27,23,31],[9,23,14,6],[21,0,27,10],[15,30,5,29],[7,6,0,3],[10,29,25,5],[13,21,30,19],[2,3,29,28],[5,13,2,29],[8,6,25,4],[4,17,24,20],[11,20,12,2],[4,19,31,8],[23,18,7,10],[24,0,8,6],[2,19,13,20],[7,21,16,17],[11,25,3,29],[7,15,11,17],[21,15,24,14],[29,24,22,13],[21,24,17,26],[12,1,24,18],[27,24,14,2],[16,28,21,10],[25,27,2,13],[22,6,18,30],[11,6,7,26],[7,10,8,28],[11,17,13,21],[11,14,21,15],[15,25,7,0],[5,23,20,7],[26,4,14,12],[31,30,26,15],[2,29,28,21],[23,8,9,28],[17,3,16,25],[27,24,23,20],[13,23,24,20],[27,20,25,15],[17,2,9,24],[29,19,28,26],[9,27,21,29],[8,27,13,15],[21,4,24,30],[18,27,9,25],[23,31,18,12],[14,2,1,19],[1,26,20,9],[25,10,18,8],[3,21,9,5],[19,15,4,5],[0,17,8,4],[3,10,12,29],[14,0,13,5],[18,27,10,25],[27,31,23,19],[7,9,31,28],[17,31,1,22],[22,18,25,10],[24,14,9,11],[12,30,0,14],[5,8,19,23],[6,30,28,9],[3,21,6,1],[23,27,3,14],[0,18,4,6],[25,28,29,30],[24,2,0,29],[25,2,8,18],[13,19,10,20],[2,18,7,0],[5,2,0,10],[19,14,4,3],[12,2,5,14],[16,22,9,30]],[[18,21,24,6],[23,3,5,4],[29,20,14,27],[3,0,13,26],[12,14,21,11],[23,13,14,5],[0,22,23,13],[27,14,25,9],[28,31,8,1],[19,25,22,14],[29,7,16,8],[30,5,22,25],[23,19,0,22],[8,6,18,30],[30,25,31,11],[6,30,13,0],[11,20,21,22],[20,23,5,2],[0,7,14,22],[13,28,21,22],[15,9,24,29],[1,15,21,9],[21,17,4,28],[8,6,15,18],[12,21,26,2],[25,2,23,12],[20,12,22,1],[20,19,6,1],[23,2,9,16],[26,28,11,10],[30,10,27,11],[28,13,1,31],[6,15,29,9],[8,21,22,28],[10,30,6,31],[22,10,18,15],[31,5,10,17],[10,27,3,9],[16,20,19,6],[12,1,9,19],[4,27,11,14],[27,10,24,3],[27,26,14,10],[10,25,1,9],[31,0,3,14],[11,17,14,15],[2,29,24,17],[0,30,5,29],[14,27,19,10],[17,23,8,19],[11,17,15,13],[15,14,10,22],[9,29,8,16],[20,16,4,24],[27,0,22,1],[2,21,28,18],[22,16,12,6],[21,30,12,31],[10,1,2,6],[20,16,6,19],[6,13,21,20],[18,10,24,21],[26,31,29,24],[11,0,23,16],[21,18,0,23],[13,0,31,28],[30,28,19,13],[12,29,2,22],[27,2,1,10],[13,30,1,3],[6,18,3,16],[18,4,28,17],[9,23,0,25],[6,24,20,26],[6,25,29,13],[6,29,8,19],[31,19,16,24],[14,27,19,21],[24,3,31,29],[17,6,27,29],[8,3,19,12],[18,26,2,20],[2,13,17,11],[3,16,30,0],[11,26,7,17],[5,13,11,21],[19,7,29,30],[25,27,9,14],[21,4,14,22],[9,17,23,4],[31,9,7,14],[3,18,22,7],[27,16,23,25],[4,2,22,15],[19,26,17,2],[23,2,27,7],[19,22,1,25],[10,26,3,25],[9,17,15,13],[7,10,18,21],[28,20,30,16],[3,23,29,5],[14,23,26,27],[20,27,8,21],[26,11,10,30],[22,30,1,17],[7,18,19,31],[9,8,4,28],[27,31,4,19],[27,4,8,11],[30,4,8,20],[5,23,13,17],[17,14,6,12],[9,3,12,21],[16,22,1,13],[30,14,27,4],[26,31,2,22],[25,23,20,2],[29,19,20,13],[11,24,4,18],[7,30,13,23],[23,21,30,7],[17,30,26,28],[2,14,8,22],[22,21,1,8],[11,26,20,8],[20,27,0,30],[29,21,2,31]],[[4,31,13,22],[26,15,17,2],[28,0,7,21],[1,25,29,8],[23,26,11,0],[17,18,29,4],[2,14,30,18],[22,13,21,7],[10,14,7,23],[2,10,17,28],[28,25,8,24],[22,19,5,27],[31,11,5,3],[26,1,0,28],[20,1,18,28],[24,4,30,13],[25,8,21,3],[29,24,26,13],[29,21,15,5],[30,5,17,12],[27,10,16,25],[7,17,27,1],[20,22,17,18],[28,4,25,14],[24,0,20,8],[31,27,11,7],[2,4,22,18],[20,9,31,2],[7,29,3,18],[19,2,20,14],[11,9,21,24],[2,20,1,25],[5,3,20,28],[21,9,20,0],[12,23,31,17],[16,18,13,2],[4,25,8,21],[9,24,3,22],[10,0,8,11],[30,28,27,23],[3,0,6,23],[0,10,29,1],[20,4,12,1],[5,23,15,11],[8,16,14,23],[11,12,6,21],[5,4,10,11],[31,3,9,21],[22,31,29,28],[20,16,27,25],[20,31,15,11],[25,2,7,10],[5,19,28,9],[9,3,19,22],[11,2,12,7],[6,30,22,17],[14,29,17,12],[20,18,8,6],[25,6,29,2],[8,6,15,29],[20,28,29,24],[7,23,21,29],[28,10,7,21],[5,0,26,14],[1,27,31,11],[21,18,9,6],[27,10,29,0],[28,15,12,18],[8,23,25,15],[18,17,1,29],[15,27,21,16],[7,19,8,20],[10,26,11,31],[28,19,6,4],[17,12,23,7],[24,0,12,20],[17,25,10,0],[4,19,13,29],[26,5,11,6],[7,3,13,21],[0,29,3,11],[7,22,5,21],[18,4,3,9],[11,25,24,10],[0,6,22,30],[15,26,14,5],[8,25,3,29],[28,18,1,29],[18,16,3,4],[4,9,26,7],[5,26,19,21],[12,19,21,31],[13,2,8,31],[3,24,7,1],[23,11,1,31],[2,12,1,25],[29,20,24,13],[23,15,17,26],[28,27,7,21],[0,23,6,30],[5,23,26,3],[9,28,20,19],[3,31,15,9],[8,29,23,0],[2,12,9,28],[27,7,22,6],[17,19,7,31],[18,17,10,7],[28,29,24,31],[0,9,11,23],[29,20,2,11],[27,28,1,9],[13,31,20,0],[1,10,25,23],[23,19,25,29],[20,7,19,11],[10,23,17,14],[1,14,18,28],[2,4,9,0],[30,29,1,20],[29,7,1,26],[4,17,22,6],[19,10,30,18],[10,22,20,15],[14,1,5,25],[21,18,8,30],[8,22,3,1],[6,26,18,28]],[[13,3,18,10],[7,13,8,18],[18,29,19,20],[24,17,22,12],[21,22,7,4],[17,11,30,2],[2,4,14,18],[6,11,19,22],[28,15,18,22],[3,1,26,24],[1,18,13,5],[0,15,12,16],[7,25,1,0],[4,18,0,15],[29,12,8,4],[28,31,6,3],[5,3,23,14],[22,24,25,27],[9,13,11,10],[13,24,23,1],[28,4,20,16],[9,30,16,4],[10,30,5,29],[15,21,17,10],[10,29,26,5],[13,30,7,4],[30,1,19,8],[19,31,11,10],[25,4,2,11],[13,7,18,10],[16,12,24,31],[24,28,1,20],[27,2,20,17],[16,13,5,31],[24,3,15,11],[22,30,15,19],[29,7,21,4],[24,7,10,14],[11,12,1,15],[29,24,16,17],[31,23,11,6],[31,2,22,11],[4,27,15,21],[25,18,4,5],[6,17,18,20],[30,22,11,19],[18,14,16,0],[21,17,9,11],[20,26,22,7],[16,31,10,13],[4,23,2,25],[19,27,6,0],[27,4,6,9],[2,19,14,30],[30,31,29,18],[16,0,10,20],[29,23,20,11],[25,15,2,31],[8,3,21,5],[6,1,30,10],[12,2,13,16],[26,20,4,14],[5,20,17,2],[4,29,16,30],[1,6,8,21],[2,18,11,19],[18,6,3,14],[24,27,17,25],[4,1,5,0],[15,17,9,3],[10,6,9,26],[5,7,14,0],[0,6,19,13],[13,17,19,24],[24,9,23,8],[3,18,8,4],[18,6,16,28],[14,4,18,5],[10,30,22,28],[8,14,26,2],[19,6,29,10],[22,15,29,17],[3,16,20,15],[6,15,11,9],[15,12,14,13],[23,25,24,4],[31,2,10,11],[20,6,27,11],[1,18,0,24],[13,19,22,25],[6,21,3,29],[16,21,11,10],[31,20,1,10],[18,28,22,6],[17,20,6,15],[16,14,4,6],[9,31,5,16],[10,6,18,25],[17,27,16,29],[2,22,5,21],[19,3,10,13],[4,23,11,16],[5,14,23,8],[23,9,17,26],[8,21,3,27],[25,0,23,18],[28,31,30,3],[0,15,12,24],[14,20,13,27],[8,19,13,16],[11,6,13,20],[2,17,29,26],[24,30,18,21],[10,11,3,20],[3,30,23,31],[17,29,10,13],[19,7,27,17],[28,13,2,9],[13,24,31,6],[28,11,24,12],[20,16,11,8],[6,20,21,26],[10,18,8,13],[23,21,12,4],[5,2,12,7],[16,2,13,14],[5,7,18,4],[6,22,23,31]],[[8,2,25,17],[20,12,25,4],[25,15,9,18],[25,21,23,9],[11,19,28,4],[25,10,14,15],[6,13,24,19],[2,13,15,14],[6,27,16,7],[15,31,9,30],[9,24,11,29],[7,31,17,30],[28,1,22,17],[28,22,21,24],[9,0,23,21],[24,31,30,3],[11,4,29,9],[16,9,22,21],[28,25,17,16],[20,28,23,11],[25,4,30,14],[22,21,20,24],[11,20,9,2],[18,21,13,5],[30,23,21,18],[10,20,26,18],[12,6,0,16],[25,20,3,26],[28,13,22,1],[2,20,26,14],[20,17,31,4],[22,13,29,23],[0,3,12,2],[25,0,22,27],[23,15,31,16],[26,30,13,22],[0,21,15,9],[10,22,8,26],[1,27,12,23],[1,14,23,8],[18,6,0,3],[4,23,27,6],[25,4,20,1],[1,0,20,17],[1,2,14,4],[23,10,21,4],[4,3,24,28],[2,25,17,27],[18,24,19,12],[12,26,5,9],[5,12,29,15],[0,30,21,26],[5,24,12,14],[2,4,25,31],[13,26,4,9],[6,7,5,29],[14,19,7,16],[26,16,18,25],[9,22,24,5],[9,12,1,26],[4,26,11,5],[29,31,22,17],[13,15,9,17],[23,25,30,6],[30,13,2,14],[12,19,2,17],[5,31,1,10],[23,11,26,0],[26,5,9,25],[20,17,25,2],[0,12,21,22],[24,22,6,28],[1,17,8,24],[27,21,26,28],[11,12,28,0],[11,4,0,9],[1,13,19,16],[12,8,18,23],[2,30,18,12],[22,26,30,13],[17,29,20,31],[4,6,12,14],[11,26,7,9],[25,15,11,8],[2,16,10,5],[17,10,1,5],[30,25,12,21],[5,10,23,28],[28,29,26,17],[21,7,22,16],[9,13,26,10],[25,13,27,9],[1,7,13,31],[23,13,21,18],[0,19,14,18],[23,8,18,27],[20,27,14,10],[11,18,29,17],[21,17,3,6],[24,23,6,8],[28,15,24,18],[23,26,5,27],[18,31,26,14],[21,27,30,2],[12,4,21,17],[18,21,8,3],[21,0,28,31],[13,25,8,30],[12,31,15,13],[9,13,26,18],[20,23,10,4],[1,19,31,24],[29,11,12,21],[9,3,21,29],[29,20,21,0],[5,13,30,4],[30,3,25,23],[9,21,1,22],[3,15,29,27],[14,26,6,23],[24,15,29,4],[31,4,6,8],[16,9,1,18],[27,16,11,19],[31,28,4,26],[26,16,20,24],[23,18,30,10],[9,14,4,3]],[[6,24,16,25],[23,11,0,19],[12,24,16,26],[0,7,22,1],[24,11,13,22],[0,8,30,16],[13,4,24,2],[9,3,28,25],[16,21,3,1],[0,9,31,8],[2,25,30,16],[11,29,5,22],[9,5,26,28],[31,9,3,10],[20,30,12,18],[9,11,25,15],[20,7,1,19],[3,6,21,9],[5,30,8,26],[10,4,11,0],[30,29,28,25],[10,11,4,28],[19,4,5,2],[10,24,28,23],[18,31,22,25],[16,31,20,28],[29,7,12,0],[6,29,10,21],[13,8,3,29],[22,11,8,6],[0,19,12,22],[18,17,21,3],[10,23,21,0],[4,23,13,27],[26,16,19,5],[25,1,4,31],[31,4,7,1],[11,8,18,1],[26,28,3,6],[11,5,8,21],[0,7,15,4],[0,30,16,23],[30,18,21,15],[20,0,27,5],[6,10,23,8],[7,8,22,15],[27,9,16,15],[18,10,21,9],[6,5,29,21],[9,8,27,12],[17,24,7,20],[25,12,7,17],[10,19,21,5],[10,20,5,17],[19,15,7,18],[9,15,23,24],[31,4,12,30],[9,6,23,17],[2,31,28,5],[23,24,18,0],[6,2,28,23],[8,23,11,6],[31,24,6,2],[18,9,17,1],[12,15,2,16],[26,19,29,11],[27,7,8,0],[10,22,5,8],[20,26,30,24],[15,3,13,12],[10,8,29,12],[6,23,10,18],[25,28,22,1],[31,8,14,13],[23,15,31,18],[15,5,28,20],[18,1,17,0],[13,16,1,26],[14,21,29,2],[26,21,3,7],[7,14,31,1],[26,10,16,12],[16,2,9,11],[6,12,17,11],[15,18,27,7],[12,19,24,25],[23,6,12,18],[15,21,25,26],[10,20,3,30],[16,25,17,1],[3,28,26,6],[31,7,8,29],[10,2,29,4],[29,27,8,23],[12,28,30,14],[14,20,13,1],[28,6,2,9],[20,27,30,5],[26,27,6,18],[1,5,30,23],[29,30,14,15],[10,5,18,2],[4,7,21,12],[31,12,18,15],[16,9,26,11],[7,8,11,28],[7,22,10,24],[0,26,23,14],[19,29,11,14],[16,18,0,5],[5,23,12,17],[27,16,25,19],[13,18,10,2],[26,19,14,20],[9,20,26,21],[28,21,30,2],[1,6,27,28],[30,4,2,26],[13,18,2,23],[30,23,18,9],[7,10,29,2],[12,4,25,11],[12,18,23,7],[3,4,11,8],[7,23,24,4],[20,5,25,26],[5,16,10,0],[14,25,22,26]],[[26,11,17,14],[14,3,9,24],[2,14,10,13],[4,24,10,22],[16,24,28,23],[19,13,0,18],[8,13,6,26],[14,13,3,27],[13,14,17,16],[11,31,5,17],[0,18,26,24],[3,27,4,22],[20,15,6,14],[20,31,18,19],[12,7,18,14],[11,18,21,26],[24,19,16,1],[11,26,1,16],[30,16,8,2],[5,15,9,25],[6,12,19,29],[29,20,15,26],[6,11,20,29],[23,27,10,15],[1,25,13,18],[31,3,9,7],[30,13,17,14],[10,23,19,12],[3,30,27,21],[8,22,18,16],[4,0,16,3],[28,22,0,5],[3,30,5,10],[0,2,15,7],[7,17,27,8],[24,25,14,7],[2,7,18,25],[16,21,10,24],[6,25,23,21],[18,31,12,17],[12,26,14,13],[26,4,1,21],[29,15,0,31],[5,8,28,2],[13,21,22,28],[24,5,14,1],[14,20,19,17],[0,18,4,27],[8,19,12,11],[18,2,10,3],[18,3,26,23],[9,18,2,31],[25,27,8,28],[7,29,14,23],[11,5,26,4],[21,16,26,2],[11,25,13,20],[4,21,19,10],[24,1,0,8],[6,16,19,5],[9,20,28,24],[6,1,13,5],[19,25,13,29],[14,4,22,23],[3,7,4,0],[9,11,27,1],[0,28,24,5],[23,17,21,0],[7,2,17,3],[11,7,0,21],[11,12,16,28],[8,16,1,4],[15,23,22,4],[3,13,25,21],[3,11,4,8],[22,1,11,9],[22,30,19,15],[17,19,15,8],[24,28,6,7],[21,8,24,23],[5,15,30,18],[31,9,16,24],[31,7,10,9],[28,10,18,23],[3,23,22,12],[24,16,18,13],[9,8,24,30],[0,29,13,1],[13,18,25,3],[22,10,28,16],[1,0,6,14],[3,28,5,30],[1,5,28,14],[6,22,8,19],[13,2,25,20],[24,27,5,11],[24,8,10,2],[7,22,0,6],[8,20,30,6],[6,5,15,4],[7,28,22,14],[21,5,6,28],[7,28,20,25],[15,20,22,17],[27,9,16,20],[20,7,2,5],[24,6,31,12],[31,22,6,13],[22,31,20,15],[15,31,25,28],[27,19,30,11],[2,14,19,0],[10,17,24,26],[1,25,23,10],[6,8,19,10],[25,17,15,30],[8,14,31,26],[12,21,30,14],[21,30,11,31],[3,19,13,6],[19,18,17,4],[25,31,10,14],[0,3,22,13],[6,21,5,1],[18,5,7,20],[8,10,18,31],[31,8,27,25],[17,30,14,23]],[[19,0,27,29],[18,14,23,27],[26,4,8,3],[19,30,4,22],[4,6,5,10],[22,30,2,23],[4,28,25,17],[11,18,19,16],[15,12,2,24],[23,10,12,21],[22,17,23,29],[6,11,22,0],[22,7,12,1],[13,22,9,4],[15,12,7,4],[21,30,13,23],[19,3,28,30],[10,5,6,16],[30,31,9,18],[19,6,22,7],[25,22,31,16],[31,13,19,22],[22,5,8,28],[14,31,27,22],[31,3,2,11],[8,17,29,21],[31,11,7,13],[23,14,25,30],[9,13,17,29],[22,31,6,10],[17,3,30,16],[0,9,19,2],[25,12,24,31],[23,26,15,16],[29,22,31,7],[25,18,4,7],[3,11,1,24],[0,27,15,19],[14,4,17,19],[30,7,6,17],[29,5,16,9],[20,11,22,7],[22,31,26,10],[7,0,5,3],[16,29,17,28],[16,21,8,12],[29,0,8,6],[30,27,5,8],[23,30,26,11],[16,4,26,21],[9,22,8,28],[19,29,16,24],[31,5,8,19],[13,15,3,26],[17,4,31,23],[2,25,12,7],[25,7,10,4],[0,7,9,25],[5,15,13,0],[8,25,30,1],[4,19,8,23],[28,19,16,18],[3,7,21,24],[8,20,2,22],[20,0,4,18],[26,23,5,16],[27,7,11,20],[30,14,23,15],[24,30,28,1],[17,2,5,27],[27,4,14,21],[25,1,13,21],[6,30,18,29],[7,15,12,17],[25,23,27,21],[20,23,5,9],[24,23,31,29],[27,25,20,4],[27,14,3,7],[22,12,31,18],[21,20,11,14],[18,27,28,3],[31,29,3,25],[11,6,3,23],[1,14,29,9],[2,26,9,7],[22,0,11,15],[21,8,14,24],[0,19,27,31],[4,29,30,12],[21,31,22,1],[26,25,0,21],[23,26,2,13],[5,3,31,14],[4,22,20,21],[26,24,30,17],[29,16,12,6],[2,12,29,16],[28,1,9,4],[23,16,11,31],[16,10,25,14],[31,6,14,30],[25,29,23,10],[17,6,30,13],[24,17,30,27],[1,6,21,18],[26,28,7,6],[30,16,3,27],[16,22,11,10],[24,31,23,16],[23,4,25,24],[11,27,1,13],[2,7,25,22],[21,22,14,5],[30,17,12,3],[3,10,20,23],[19,22,2,1],[27,6,4,18],[18,10,2,4],[4,9,25,30],[22,29,28,4],[27,25,31,14],[25,13,28,10],[28,27,8,12],[11,30,16,31],[31,19,4,5],[19,3,26,16],[22,31,26,7]],[[25,3,18,28],[24,17,16,22],[29,22,6,28],[18,6,19,10],[7,15,12,5],[20,18,8,17],[20,7,16,18],[21,3,29,30],[13,23,24,25],[13,24,10,11],[9,0,27,4],[14,13,24,27],[6,2,4,25],[24,31,7,30],[17,24,8,26],[18,14,23,16],[2,17,27,21],[1,20,16,23],[6,7,30,8],[9,3,1,29],[21,10,1,7],[26,21,11,10],[9,18,28,15],[27,25,29,20],[24,5,3,12],[30,13,4,20],[14,9,23,19],[14,21,2,12],[9,13,10,22],[16,19,2,31],[25,18,22,13],[26,23,12,28],[29,20,16,4],[31,6,27,5],[6,4,17,24],[8,3,26,25],[19,30,6,15],[31,23,25,0],[11,13,18,28],[24,8,17,30],[9,25,11,15],[16,4,1,15],[28,17,23,19],[18,15,7,9],[28,13,8,9],[11,22,25,5],[27,6,0,28],[28,30,9,29],[22,4,17,13],[15,30,6,9],[27,12,28,19],[17,21,31,18],[19,24,25,26],[23,8,14,2],[2,26,18,24],[23,22,31,16],[5,12,4,26],[30,3,22,17],[10,12,0,22],[18,7,26,6],[27,18,26,11],[26,8,15,23],[10,21,0,16],[11,4,1,5],[21,15,1,16],[16,7,29,11],[19,7,16,1],[18,23,10,2],[30,6,20,3],[10,13,7,20],[12,23,9,22],[14,4,6,28],[13,29,31,3],[30,3,31,9],[7,11,17,8],[14,6,2,10],[26,18,31,16],[14,21,24,1],[14,10,8,4],[26,20,17,23],[15,30,27,22],[24,31,9,4],[29,22,10,15],[18,26,2,12],[15,8,1,3],[2,10,22,26],[8,23,29,16],[14,12,22,26],[10,8,15,14],[31,13,27,11],[3,22,17,19],[12,2,1,23],[16,12,13,7],[5,6,23,12],[23,25,3,21],[11,21,22,31],[17,21,31,6],[16,10,29,26],[7,13,21,5],[15,12,0,23],[12,17,31,1],[19,22,18,4],[8,6,7,21],[7,18,17,8],[21,26,9,22],[15,22,20,4],[17,6,29,22],[4,20,16,29],[29,9,26,13],[20,7,24,9],[4,18,14,30],[5,1,29,3],[24,4,8,18],[23,6,20,11],[12,22,17,15],[7,0,3,11],[19,18,28,21],[7,12,14,16],[5,29,25,27],[25,7,11,13],[12,24,19,22],[0,11,15,12],[11,25,29,22],[10,16,14,3],[1,12,18,4],[28,5,1,17],[28,30,24,23],[28,30,17,31]],[[24,7,14,8],[6,20,30,15],[21,1,29,20],[23,20,24,18],[13,0,6,4],[26,19,3,25],[28,23,19,24],[30,15,21,14],[31,10,0,2],[24,20,18,7],[30,5,17,21],[24,12,23,25],[26,15,25,20],[3,28,26,9],[18,7,17,16],[25,5,8,7],[24,15,18,9],[11,30,29,12],[28,29,22,2],[8,18,21,10],[9,2,4,5],[1,29,20,8],[5,4,26,27],[3,19,2,8],[4,1,29,15],[13,18,21,3],[2,22,12,18],[27,14,9,21],[28,27,30,16],[16,26,20,13],[31,20,13,27],[6,26,7,21],[22,10,30,20],[23,31,20,11],[14,9,13,2],[2,19,22,12],[9,31,22,29],[8,27,1,30],[28,20,5,0],[14,24,20,13],[26,11,31,16],[18,30,19,23],[18,30,7,27],[25,11,8,15],[31,27,9,26],[20,14,0,8],[30,18,14,22],[31,15,16,4],[28,15,19,6],[23,13,31,12],[29,26,28,9],[28,3,16,15],[20,4,10,15],[2,29,27,31],[31,13,16,23],[9,12,2,17],[23,19,8,6],[30,3,17,20],[26,19,2,27],[22,16,10,27],[19,25,1,10],[24,25,2,17],[3,12,30,16],[16,17,25,3],[25,12,14,4],[17,16,3,18],[15,24,5,16],[16,12,4,29],[4,17,28,1],[21,2,25,6],[9,15,1,28],[20,12,23,30],[10,19,2,14],[11,14,2,17],[16,28,5,8],[16,13,19,25],[11,27,18,3],[10,20,13,31],[31,14,21,30],[7,25,17,27],[24,22,14,12],[3,4,23,15],[3,6,17,22],[12,21,2,1],[1,19,16,14],[9,11,25,1],[17,25,12,24],[31,27,25,15],[25,14,8,4],[18,14,11,20],[5,0,21,15],[14,10,17,25],[3,19,0,1],[9,3,10,6],[3,4,28,2],[3,7,22,14],[26,16,20,8],[23,14,9,26],[10,0,29,11],[25,31,22,6],[15,17,21,1],[31,16,27,26],[6,24,11,27],[4,5,21,24],[31,5,10,13],[7,14,20,10],[5,9,18,21],[2,6,11,10],[25,29,30,5],[13,24,15,30],[17,20,1,5],[30,29,25,6],[19,11,13,3],[19,26,22,11],[15,3,30,9],[8,26,3,11],[27,15,31,1],[28,3,20,22],[25,18,3,2],[17,3,31,9],[22,29,24,26],[26,16,15,0],[29,9,11,24],[5,13,4,14],[15,26,31,12],[12,29,15,7],[0,31,18,6],[9,10,6,30]],[[18,8,10,29],[14,3,2,6],[29,4,30,9],[0,21,17,15],[0,25,4,22],[1,30,21,10],[9,11,18,27],[5,19,9,15],[3,2,5,21],[5,6,11,19],[18,13,16,5],[4,22,27,24],[24,4,10,19],[1,29,16,3],[13,6,8,14],[3,26,19,30],[3,19,25,18],[24,9,16,18],[29,25,24,28],[21,8,1,15],[8,11,27,9],[31,28,21,27],[30,10,1,13],[25,4,14,23],[24,23,29,27],[13,28,26,12],[18,0,21,27],[11,21,27,31],[28,10,5,21],[1,22,13,4],[8,3,27,16],[3,8,1,18],[13,10,21,0],[4,6,21,5],[7,31,15,5],[15,25,0,4],[18,4,29,23],[1,16,20,13],[25,22,31,24],[3,8,18,29],[23,4,14,19],[12,15,23,10],[10,12,8,30],[5,26,15,25],[3,1,11,26],[1,18,16,11],[30,2,21,13],[11,24,13,7],[25,28,9,8],[7,14,1,9],[5,11,3,8],[2,15,30,1],[11,22,6,27],[10,12,18,1],[21,1,22,8],[28,8,4,31],[6,16,27,31],[25,13,23,26],[29,24,16,20],[26,7,30,25],[13,15,25,26],[6,13,22,4],[11,4,29,5],[12,28,26,21],[27,25,22,15],[31,14,19,25],[21,12,16,9],[0,9,11,20],[18,22,26,14],[1,7,29,8],[25,10,12,2],[27,3,14,9],[2,20,25,8],[21,7,10,6],[22,7,18,17],[10,18,4,1],[6,16,17,3],[15,4,24,11],[5,12,17,1],[10,13,21,4],[29,14,10,3],[11,0,4,28],[27,17,14,13],[6,13,24,3],[11,29,13,23],[11,22,8,2],[0,27,18,7],[21,16,12,6],[16,12,4,25],[29,23,22,31],[4,21,23,8],[6,13,1,31],[21,20,30,18],[20,10,18,24],[21,2,3,4],[6,3,16,7],[26,1,30,19],[19,5,10,25],[11,25,16,26],[0,28,12,27],[28,16,25,2],[17,3,0,19],[18,25,13,11],[7,3,25,0],[12,14,5,22],[9,7,29,13],[2,25,15,17],[4,1,11,23],[28,18,7,10],[8,27,28,13],[24,1,4,25],[12,28,29,15],[15,16,12,14],[14,2,0,29],[21,27,11,7],[27,25,7,22],[19,8,28,24],[20,27,2,15],[29,0,19,15],[9,6,10,11],[19,4,15,22],[11,7,24,18],[0,31,23,2],[16,2,21,29],[21,23,15,31],[19,4,16,11],[23,27,9,10],[24,11,13,18]],[[29,31,5,20],[14,5,12,20],[18,9,10,3],[30,7,11,10],[8,0,6,9],[22,25,18,4],[23,31,26,18],[15,18,29,17],[26,23,29,30],[12,18,28,7],[0,12,28,27],[9,8,3,29],[0,10,29,21],[24,19,7,30],[1,10,7,5],[0,24,17,25],[9,13,27,15],[20,4,8,14],[13,2,8,14],[6,29,10,19],[21,27,12,19],[23,5,13,11],[31,27,10,24],[20,14,15,18],[7,10,3,17],[21,18,29,4],[22,2,12,27],[24,25,30,9],[7,24,11,30],[30,26,17,2],[5,3,21,13],[3,26,18,6],[15,29,6,8],[15,30,9,24],[1,4,12,6],[21,25,18,9],[17,24,15,13],[29,7,6,14],[17,14,27,10],[30,8,0,12],[10,16,12,25],[16,21,29,0],[27,5,25,19],[7,29,18,23],[19,5,15,4],[5,21,17,7],[28,8,17,22],[5,4,6,7],[10,5,29,7],[15,28,26,11],[26,2,22,11],[8,31,28,18],[22,27,17,10],[19,1,23,29],[23,21,31,6],[12,31,0,8],[10,22,20,2],[30,5,6,15],[15,16,22,31],[28,3,7,17],[10,30,6,22],[15,13,29,28],[16,9,27,31],[18,28,15,14],[5,23,31,12],[12,10,6,24],[13,8,18,1],[10,15,1,26],[19,12,16,14],[10,28,13,31],[10,0,30,9],[12,30,24,10],[1,16,25,0],[17,21,5,12],[9,10,8,13],[9,29,4,19],[23,17,29,16],[30,2,12,11],[4,13,3,6],[5,22,2,14],[11,16,24,22],[22,11,8,20],[25,27,10,13],[11,1,18,0],[28,2,4,27],[2,11,13,31],[10,26,16,6],[17,22,9,5],[16,31,12,8],[24,3,31,26],[19,26,9,13],[2,17,14,4],[5,13,29,10],[22,2,10,7],[6,14,19,17],[16,21,0,31],[28,18,26,8],[31,24,16,29],[31,28,30,2],[3,31,17,0],[14,5,28,31],[4,23,21,9],[15,12,23,0],[9,1,29,15],[19,22,29,8],[10,6,13,12],[19,15,11,27],[4,20,27,0],[9,27,4,5],[31,20,18,29],[5,4,22,29],[5,19,27,8],[31,2,8,7],[30,2,11,8],[21,5,6,18],[11,5,24,17],[23,31,11,4],[10,23,16,26],[4,5,27,1],[6,16,5,17],[16,12,22,26],[1,17,9,3],[12,13,5,15],[11,9,16,27],[21,8,19,1],[1,2,4,3],[9,20,11,27],[28,3,31,30]],[[27,19,2,25],[14,31,13,30],[25,14,23,10],[22,28,5,0],[21,24,29,9],[31,15,18,23],[14,15,18,9],[15,1,27,17],[0,17,24,4],[28,24,13,26],[31,8,6,9],[26,1,8,28],[10,26,14,21],[22,8,1,10],[13,4,10,23],[13,2,12,16],[16,29,18,28],[22,17,15,5],[5,8,2,1],[31,3,22,29],[28,22,20,3],[26,17,30,8],[28,18,9,12],[21,7,6,2],[6,1,13,25],[17,6,10,26],[1,4,19,3],[17,23,7,9],[6,0,28,29],[10,17,20,6],[16,29,30,14],[7,9,29,17],[13,25,4,27],[27,14,2,9],[2,28,1,10],[25,12,27,18],[9,3,16,18],[3,18,22,10],[23,2,5,8],[5,26,25,1],[5,16,8,11],[7,10,6,14],[28,20,31,13],[18,30,12,10],[20,19,12,4],[20,30,26,24],[10,30,11,9],[19,15,20,3],[16,9,7,17],[19,10,20,18],[17,27,7,5],[5,0,15,3],[12,6,21,28],[0,12,17,29],[22,13,25,8],[27,3,15,2],[10,0,5,7],[1,14,25,8],[31,6,30,29],[23,14,20,25],[15,23,8,17],[5,1,10,25],[17,16,7,0],[4,5,12,30],[24,10,31,28],[26,7,30,15],[23,28,27,26],[7,13,19,27],[7,30,31,28],[23,15,0,10],[9,11,23,8],[0,16,6,17],[31,17,19,15],[9,19,31,16],[13,4,31,8],[15,0,3,21],[2,31,18,1],[29,8,17,5],[23,18,26,15],[19,0,9,24],[18,10,6,21],[15,19,21,18],[8,16,20,10],[21,3,0,19],[9,30,15,14],[16,0,28,11],[8,6,18,24],[17,6,9,11],[31,16,28,8],[19,0,23,21],[7,30,18,11],[6,7,22,19],[12,6,30,15],[21,27,30,20],[24,7,17,18],[8,1,11,17],[22,31,16,21],[13,24,20,29],[26,30,19,29],[20,6,8,21],[17,10,24,12],[19,17,4,12],[28,17,30,23],[15,19,11,10],[29,23,24,8],[13,21,14,22],[4,22,6,24],[27,1,10,29],[2,21,24,7],[11,16,2,22],[21,28,15,8],[0,15,30,12],[9,17,2,11],[9,1,15,8],[10,29,2,20],[15,12,30,21],[8,0,10,19],[30,1,22,19],[14,29,28,15],[2,30,15,14],[6,22,2,15],[12,14,11,25],[15,8,26,13],[4,2,14,18],[4,21,17,26],[8,23,22,6],[17,27,28,19],[10,6,29,21]],[[15,0,16,29],[29,0,2,9],[0,31,6,7],[29,19,18,13],[24,29,5,28],[1,2,6,16],[17,7,8,29],[18,7,27,24],[0,6,5,20],[13,1,4,28],[18,31,12,15],[0,18,27,19],[15,11,4,27],[1,26,5,24],[29,15,4,20],[12,20,18,17],[8,26,22,2],[26,19,1,14],[13,10,20,11],[24,11,17,1],[5,11,2,12],[25,22,18,7],[3,23,14,31],[24,25,13,31],[19,28,22,6],[11,31,23,20],[18,26,17,12],[4,6,10,20],[24,5,26,22],[23,5,12,28],[11,25,27,1],[27,0,2,12],[22,14,7,6],[19,1,24,12],[2,31,17,22],[10,18,29,14],[12,10,11,31],[11,25,3,10],[22,15,6,1],[27,0,4,25],[31,21,17,13],[17,19,21,9],[14,25,7,1],[24,16,17,2],[12,7,5,27],[12,22,19,29],[1,0,30,3],[28,8,9,13],[29,28,8,4],[11,23,3,4],[2,30,15,6],[1,28,18,17],[3,8,11,20],[16,1,8,15],[19,10,24,8],[5,29,19,25],[14,21,15,0],[5,3,19,24],[11,2,13,28],[14,0,31,26],[10,5,0,19],[12,2,28,9],[22,25,27,18],[3,6,21,10],[26,16,14,11],[24,0,17,7],[29,4,18,20],[19,12,1,23],[1,11,23,10],[22,15,13,21],[22,3,5,0],[7,26,3,29],[3,31,19,6],[7,5,19,29],[5,30,14,31],[16,29,27,5],[0,11,21,30],[13,3,31,10],[7,30,3,19],[21,8,23,0],[10,24,8,18],[23,25,9,6],[8,16,11,22],[14,22,30,28],[25,20,12,13],[23,8,4,3],[10,22,16,29],[3,18,24,4],[28,16,7,30],[27,28,5,20],[7,4,23,0],[17,3,21,26],[21,31,20,3],[15,2,5,29],[1,14,7,0],[22,2,31,15],[10,20,16,19],[12,14,7,18],[30,14,20,31],[30,7,17,9],[18,24,14,3],[3,12,29,15],[14,13,2,21],[8,7,31,30],[7,23,22,6],[0,24,3,7],[21,4,0,16],[1,23,16,18],[7,11,17,3],[29,30,15,24],[8,22,18,31],[14,7,28,13],[4,22,8,19],[1,11,10,3],[15,7,21,11],[27,28,23,26],[8,6,16,31],[10,8,6,9],[28,14,24,16],[21,16,0,4],[2,31,0,23],[23,31,6,9],[3,22,16,0],[2,22,29,1],[9,30,4,21],[22,17,20,9],[26,19,2,7],[26,11,17,5]]]
YW = 549
def setup_inputs(rng):
    return {"x": rng.standard_normal((N, 128, T), dtype=np.float32)}
def reference(x):
    y = np.full((N, 128, YW), np.nan, x.dtype)
    fill = [0] * N
    for r in range(N):
        for t in range(T):
            for e in ROUTE[r][t]:
                y[e][:, fill[e]] = x[r][:, t]
                fill[e] += 1
    return {"y": y}

@@ -1,0 +1,216 @@
+K = 8
+HOSTS = 4
+
+W_CB, W_SW, W_DS, W_DC, W_ST, W_Y = 128, 128, 128, 128, 512, 549
+SCRATCH = {
+    "xs": ("sbuf", [128, 128], "float32"),
+    "pcb": ("sbuf", [128, W_CB], "float32"),
+    "psw": ("sbuf", [128, W_SW], "float32"),
+    "rc": ("sbuf", [128, W_CB], "float32"),
+    "rm": ("sbuf", [128, W_SW], "float32"),
+    "rds": ("sbuf", [128, W_DS], "float32"),
+    "rdc": ("sbuf", [128, W_DC], "float32"),
+    "stage": ("sbuf", [128, W_ST], "float32"),
+    "ybuf": ("sbuf", [128, W_Y], "float32"),
+}
+SEMAPHORES = ["ld", "pkc", "pks", "arrc", "arrm", "arrds", "arrdc", "ga0", "ga1", "ga2", "ga3", "arrp", "sent", "st"]
+
+_CACHE = {}
+
+
+def mate_host(h):
+    return h ^ 1
+
+
+def cable_host(h):
+    return 3 - h
+
+
+def diag_host(h):
+    return (h + 2) % 4
+
+
+def make_plan(route, ntok):
+    n = len(route)
+    plan = {"cb": [], "sw": [], "cbf": [], "swf": [], "cbpos": [], "swpos": []}
+    for s in range(n):
+        h = s // K
+        m, c, d = mate_host(h), cable_host(h), diag_host(h)
+        seg = {"ca": [], "cb": [], "cc": [], "ma": [], "mb": [], "mc": []}
+        flip = 0
+        for t in range(ntok):
+            hs = set(e // K for e in route[s][t])
+            if c in hs:
+                seg["cb" if d in hs else "ca"].append(t)
+                if m in hs:
+                    seg["ma"].append(t)
+            elif m in hs:
+                seg["mb" if d in hs else "ma"].append(t)
+            elif d in hs:
+                seg["cc" if flip == 0 else "mc"].append(t)
+                flip ^= 1
+        cb = seg["ca"] + seg["cb"] + seg["cc"]
+        sw = seg["ma"] + seg["mb"] + seg["mc"]
+        plan["cb"].append(cb)
+        plan["sw"].append(sw)
+        plan["cbf"].append(len(seg["ca"]))
+        plan["swf"].append(len(seg["ma"]))
+        plan["cbpos"].append(dict((t, i) for i, t in enumerate(cb)))
+        plan["swpos"].append(dict((t, i) for i, t in enumerate(sw)))
+    toks = [[[] for e in range(n)] for s in range(n)]
+    for s in range(n):
+        for t in range(ntok):
+            for e in route[s][t]:
+                toks[s][e].append(t)
+    off = [[0] * n for s in range(n)]
+    tot = [0] * n
+    for e in range(n):
+        for s in range(n):
+            off[s][e] = tot[e]
+            tot[e] += len(toks[s][e])
+    plan["toks"], plan["off"], plan["tot"] = toks, off, tot
+    return plan
+
+
+def runs(pairs):
+    out = []
+    for b, p in pairs:
+        if out and out[-1][0] == b and out[-1][1] + out[-1][2] == p:
+            out[-1][2] += 1
+        else:
+            out.append([b, p, 1])
+    return out
+
+
+def popcount(x):
+    return bin(x).count("1")
+
+
+def rank_program(g, core, T, topo):
+    rank = T.rank_of(core)
+    if rank is None:
+        return
+    if "plan" not in _CACHE:
+        _CACHE["plan"] = make_plan(T.tables["ROUTE"], T.tables["T"])
+    P = _CACHE["plan"]
+    sem = T.sem
+    h, k = rank // K, rank % K
+    rm_, rc_, rd_ = mate_host(h) * K + k, cable_host(h) * K + k, diag_host(h) * K + k
+    core_m, core_c = T.cores[rm_], T.cores[rc_]
+    queues = [g.sync, g.scalar]
+    turn = [0]
+    sent = [0]
+
+    def both_wait(s, v):
+        for q in queues:
+            q.wait_ge(s, v)
+
+    def copy(out, in_, s):
+        q = queues[turn[0]]
+        turn[0] ^= 1
+        q.dma_start(out, in_).then_inc(s, 16)
+        return 16
+
+    def write(dst_core, out, in_, rsem):
+        rid, pid = topo.addr(dst_core, core)
+        mask = topo.mask(core, dst_core)
+        g.remote_dma(out, in_, rsem, sem.sent, pid, rid, mask)
+        sent[0] += popcount(mask)
+
+    g.sync.dma_start(T.xs[:], T.x[:]).then_inc(sem.ld, 16)
+    both_wait(sem.ld, 16)
+
+    def pack(buf, order, s):
+        n, j = 0, 0
+        for b, p, ln in runs([("xs", t) for t in order]):
+            n += copy(buf[:, j:j + ln], T.xs[:, p:p + ln], s)
+            j += ln
+        return n
+
+    cb, sw = P["cb"][rank], P["sw"][rank]
+    assert len(cb) <= W_CB and len(sw) <= W_SW
+    n_pkc = pack(T.pcb, cb, sem.pkc)
+    n_pks = pack(T.psw, sw, sem.pks)
+
+    if cb:
+        g.wait_ge(sem.pkc, n_pkc)
+        write(core_c, T.rc[:, 0:len(cb)], T.pcb[:, 0:len(cb)], sem.arrc)
+    if sw:
+        g.wait_ge(sem.pks, n_pks)
+        write(core_m, T.rm[:, 0:len(sw)], T.psw[:, 0:len(sw)], sem.arrm)
+
+    in_c, in_cf = len(P["cb"][rc_]), P["cbf"][rc_]
+    in_m, in_mf = len(P["sw"][rm_]), P["swf"][rm_]
+    in_ds = len(P["cb"][rd_]) - P["cbf"][rd_]
+    in_dc = len(P["sw"][rd_]) - P["swf"][rd_]
+    assert in_ds <= W_DS and in_dc <= W_DC
+    off_chip = popcount(topo.mask(core, core_c))
+
+    if in_c:
+        g.wait_ge(sem.arrc, off_chip)
+        if in_c > in_cf:
+            write(core_m, T.rds[:, 0:in_c - in_cf], T.rc[:, in_cf:in_c], sem.arrds)
+    if in_m:
+        g.wait_ge(sem.arrm, off_chip)
+        if in_m > in_mf:
+            write(core_c, T.rdc[:, 0:in_m - in_mf], T.rm[:, in_mf:in_m], sem.arrdc)
+
+    def where(s, t):
+        if s == rank:
+            return ("xs", t)
+        if s == rm_:
+            return ("rm", P["swpos"][s][t])
+        if s == rc_:
+            return ("rc", P["cbpos"][s][t])
+        p = P["cbpos"][s].get(t, -1)
+        if p >= P["cbf"][s]:
+            return ("rds", p - P["cbf"][s])
+        return ("rdc", P["swpos"][s][t] - P["swf"][s])
+
+    st_col = [0]
+    groups = [(rank, sem.ga0, []), (rm_, sem.ga1, [(sem.arrm, in_m)]), (rc_, sem.ga2, [(sem.arrc, in_c)]),
+              (rd_, sem.ga3, [(sem.arrds, in_ds), (sem.arrdc, in_dc)])]
+    deliveries = []
+    for s, gsem, needs in groups:
+        for a, width in needs:
+            if width:
+                both_wait(a, off_chip)
+        n = 0
+        pieces = []
+        for e in range(h * K, h * K + K):
+            toks = P["toks"][s][e]
+            if not toks:
+                continue
+            if e == rank:
+                buf, j = T.ybuf, P["off"][s][e]
+            else:
+                buf, j = T.stage, st_col[0]
+                pieces.append((e, j, len(toks)))
+                st_col[0] += len(toks)
+            for b, p, ln in runs([where(s, t) for t in toks]):
+                n += copy(buf[:, j:j + ln], T[b][:, p:p + ln], gsem)
+                j += ln
+        deliveries.append((s, gsem, n, pieces))
+    assert st_col[0] <= W_ST
+    for s, gsem, n, pieces in deliveries:
+        if n:
+            g.wait_ge(gsem, n)
+        for e, j, ln in pieces:
+            o = P["off"][s][e]
+            write(T.cores[e], T.ybuf[:, o:o + ln], T.stage[:, j:j + ln], sem.arrp)
+
+    n_in = 0
+    for gw in range(h * K, h * K + K):
+        if gw == rank:
+            continue
+        kk = gw % K
+        for hh in range(HOSTS):
+            if P["toks"][hh * K + kk][rank]:
+                n_in += popcount(topo.mask(T.cores[gw], core))
+    if n_in:
+        g.wait_ge(sem.arrp, n_in)
+    tot = P["tot"][rank]
+    assert tot <= W_Y
+    g.dma_start(T.y[:, 0:tot], T.ybuf[:, 0:tot]).then_inc(sem.st, 16)
+    g.wait_ge(sem.st, 16)
+    g.wait_ge(sem.sent, sent[0])

@@ -1,3 +1,5 @@
+import numpy as np
+
 K = 8
 HOSTS = 4
 
@@ -30,46 +32,8 @@ def diag_host(h):
     return (h + 2) % 4
 
 
-def make_plan(route, ntok):
-    n = len(route)
-    plan = {"cb": [], "sw": [], "cbf": [], "swf": [], "cbpos": [], "swpos": []}
-    for s in range(n):
-        h = s // K
-        m, c, d = mate_host(h), cable_host(h), diag_host(h)
-        seg = {"ca": [], "cb": [], "cc": [], "ma": [], "mb": [], "mc": []}
-        flip = 0
-        for t in range(ntok):
-            hs = set(e // K for e in route[s][t])
-            if c in hs:
-                seg["cb" if d in hs else "ca"].append(t)
-                if m in hs:
-                    seg["ma"].append(t)
-            elif m in hs:
-                seg["mb" if d in hs else "ma"].append(t)
-            elif d in hs:
-                seg["cc" if flip == 0 else "mc"].append(t)
-                flip ^= 1
-        cb = seg["ca"] + seg["cb"] + seg["cc"]
-        sw = seg["ma"] + seg["mb"] + seg["mc"]
-        plan["cb"].append(cb)
-        plan["sw"].append(sw)
-        plan["cbf"].append(len(seg["ca"]))
-        plan["swf"].append(len(seg["ma"]))
-        plan["cbpos"].append(dict((t, i) for i, t in enumerate(cb)))
-        plan["swpos"].append(dict((t, i) for i, t in enumerate(sw)))
-    toks = [[[] for e in range(n)] for s in range(n)]
-    for s in range(n):
-        for t in range(ntok):
-            for e in route[s][t]:
-                toks[s][e].append(t)
-    off = [[0] * n for s in range(n)]
-    tot = [0] * n
-    for e in range(n):
-        for s in range(n):
-            off[s][e] = tot[e]
-            tot[e] += len(toks[s][e])
-    plan["toks"], plan["off"], plan["tot"] = toks, off, tot
-    return plan
+def popcount(x):
+    return bin(x).count("1")
 
 
 def runs(pairs):
@@ -82,8 +46,239 @@ def runs(pairs):
     return out
 
 
-def popcount(x):
-    return bin(x).count("1")
+def assign_max(w):
+    n = w.shape[0]
+    cost = (w.max() - w).astype(np.float64)
+    big = 1e18
+    u, v = np.zeros(n + 1), np.zeros(n + 1)
+    p, way = np.zeros(n + 1, dtype=np.int64), np.zeros(n + 1, dtype=np.int64)
+    for i in range(1, n + 1):
+        p[0] = i
+        j0 = 0
+        minv = np.full(n + 1, big)
+        used = np.zeros(n + 1, dtype=bool)
+        while True:
+            used[j0] = True
+            i0 = p[j0]
+            cur = cost[i0 - 1] - u[i0] - v[1:]
+            free = ~used[1:]
+            better = free & (cur < minv[1:])
+            minv[1:][better] = cur[better]
+            way[1:][better] = j0
+            cand = np.where(free, minv[1:], big)
+            j1 = int(np.argmin(cand)) + 1
+            delta = cand[j1 - 1]
+            u[p[used]] += delta
+            v[used] -= delta
+            minv[1:][free] -= delta
+            j0 = j1
+            if p[j0] == 0:
+                break
+        while j0 != 0:
+            j1 = way[j0]
+            p[j0] = p[j1]
+            j0 = j1
+    col = [0] * n
+    for j in range(1, n + 1):
+        col[p[j] - 1] = j - 1
+    return col
+
+
+def chain(seg, lists):
+    n = len(seg)
+    if n < 2:
+        return list(seg)
+    idx = dict((t, i) for i, t in enumerate(seg))
+    w = np.zeros((n, n))
+    for t in seg:
+        if t + 1 in idx:
+            w[idx[t], idx[t + 1]] += 1
+    for lst in lists:
+        for a, b in zip(lst, lst[1:]):
+            if a in idx and b in idx and a < b:
+                w[idx[a], idx[b]] += 1
+    col = assign_max(w)
+    nxt, has_pred = {}, set()
+    for i in range(n):
+        if w[i, col[i]] > 0:
+            nxt[seg[i]] = seg[col[i]]
+            has_pred.add(seg[col[i]])
+    out = []
+    for t in seg:
+        if t not in has_pred:
+            out.append(t)
+            while out[-1] in nxt:
+                out.append(nxt[out[-1]])
+    return out
+
+
+def links_of(s, via_c):
+    h, k = s // K, s % K
+    if via_c:
+        return (h, k // 2), (cable_host(h), k // 4)
+    return (mate_host(h), k // 2), (h, k // 4)
+
+
+def make_plan(route, ntok):
+    n = len(route)
+    toks = [[[] for e in range(n)] for s in range(n)]
+    for s in range(n):
+        for t in range(ntok):
+            for e in route[s][t]:
+                toks[s][e].append(t)
+    off = [[0] * n for s in range(n)]
+    tot = [0] * n
+    for e in range(n):
+        for s in range(n):
+            off[s][e] = tot[e]
+            tot[e] += len(toks[s][e])
+
+    segs = [dict((x, []) for x in ("ca", "cb", "cc", "ma", "mb", "mc")) for s in range(n)]
+    cable = dict(((h, p), 0) for h in range(HOSTS) for p in range(K // 2))
+    port = dict(((h, q), 0) for h in range(HOSTS) for q in range(2))
+    loose = []
+    for s in range(n):
+        h, k = s // K, s % K
+        m, c, d = mate_host(h), cable_host(h), diag_host(h)
+        for t in range(ntok):
+            hs = set(e // K for e in route[s][t])
+            if c in hs:
+                segs[s]["cb" if d in hs else "ca"].append(t)
+                cable[(h, k // 2)] += 1
+                if d in hs:
+                    port[(c, k // 4)] += 1
+                if m in hs:
+                    segs[s]["ma"].append(t)
+                    port[(h, k // 4)] += 1
+            elif m in hs:
+                segs[s]["mb" if d in hs else "ma"].append(t)
+                port[(h, k // 4)] += 1
+                if d in hs:
+                    cable[(m, k // 2)] += 1
+            elif d in hs:
+                loose.append((s, t))
+
+    mean_c = (sum(cable.values()) + len(loose)) / float(len(cable))
+    mean_p = (sum(port.values()) + len(loose)) / float(len(port))
+
+    def price(s, via_c):
+        a, b = links_of(s, via_c)
+        return (((cable[a] + 1) / mean_c) ** 8 - (cable[a] / mean_c) ** 8
+                + ((port[b] + 1) / mean_p) ** 8 - (port[b] / mean_p) ** 8)
+
+    def load(s, via_c, x):
+        a, b = links_of(s, via_c)
+        cable[a] += x
+        port[b] += x
+
+    way = {}
+    for s, t in loose:
+        way[(s, t)] = price(s, True) <= price(s, False)
+        load(s, way[(s, t)], 1)
+    for sweep in range(20):
+        moved = False
+        for s, t in loose:
+            v = way[(s, t)]
+            load(s, v, -1)
+            if price(s, not v) < price(s, v) - 1e-12:
+                v = not v
+                moved = True
+            way[(s, t)] = v
+            load(s, v, 1)
+        if not moved:
+            break
+    for s, t in loose:
+        segs[s]["cc" if way[(s, t)] else "mc"].append(t)
+
+    plan = {"toks": toks, "off": off, "tot": tot, "cb": [], "sw": [], "cbf": [], "swf": [], "cbpos": [], "swpos": [],
+            "cable": cable, "port": port}
+    for s in range(n):
+        h = s // K
+        m, c, d = mate_host(h), cable_host(h), diag_host(h)
+
+        def lists(hosts):
+            return [toks[s][e] for e in range(n) if e // K in hosts]
+
+        sg = segs[s]
+        cb = chain(sg["ca"], lists([c])) + chain(sg["cb"], lists([c, d])) + chain(sg["cc"], lists([d]))
+        sw = chain(sg["ma"], lists([m])) + chain(sg["mb"], lists([m, d])) + chain(sg["mc"], lists([d]))
+        plan["cb"].append(cb)
+        plan["sw"].append(sw)
+        plan["cbf"].append(len(sg["ca"]))
+        plan["swf"].append(len(sg["ma"]))
+        plan["cbpos"].append(dict((t, i) for i, t in enumerate(cb)))
+        plan["swpos"].append(dict((t, i) for i, t in enumerate(sw)))
+    choose_gateways(plan, n)
+    return plan
+
+
+def where(plan, s, host, t):
+    h = s // K
+    if host == h:
+        return ("xs", t)
+    if host == mate_host(h):
+        return ("rm", plan["swpos"][s][t])
+    if host == cable_host(h):
+        return ("rc", plan["cbpos"][s][t])
+    p = plan["cbpos"][s].get(t, -1)
+    if p >= plan["cbf"][s]:
+        return ("rds", p - plan["cbf"][s])
+    return ("rdc", plan["swpos"][s][t] - plan["swf"][s])
+
+
+def gather_of(plan, s, host, kg):
+    staged, pieces, own = [], [], []
+    for e in range(host * K, host * K + K):
+        cols = [where(plan, s, host, t) for t in plan["toks"][s][e]]
+        if e == host * K + kg:
+            own = cols
+        elif cols:
+            pieces.append((e, len(staged), len(cols)))
+            staged += cols
+    return staged, pieces, own
+
+
+def choose_gateways(plan, n):
+    memo = {}
+
+    def cost(s, host, kg):
+        if (s, host, kg) not in memo:
+            staged, pieces, own = gather_of(plan, s, host, kg)
+            memo[(s, host, kg)] = len(runs(staged)) + len(runs(own))
+        return memo[(s, host, kg)]
+
+    gw = [dict() for s in range(n)]
+    for h in range(HOSTS):
+        m, c, d = mate_host(h), cable_host(h), diag_host(h)
+        fixed = []
+        for k in range(K):
+            s = h * K + k
+            gw[s][h] = k
+            fixed.append(len(runs([("xs", t) for t in plan["cb"][s]])) + len(runs([("xs", t) for t in plan["sw"][s]]))
+                         + cost(s, h, k))
+        last = sorted(((cost(d * K + k, h, k), k) for k in range(K)), reverse=True)
+        best = None
+        for swaps in range(1 << K):
+            work = list(fixed)
+            for k in range(K):
+                km, kc = k ^ ((swaps >> (k // 2)) & 1), k ^ ((swaps >> (4 + k // 2)) & 1)
+                work[km] += cost(m * K + k, h, km)
+                work[kc] += cost(c * K + k, h, kc)
+            order = sorted(range(K), key=lambda q: work[q])
+            top = max(work[q] + last[i][0] for i, q in enumerate(order))
+            if best is None or top < best[0]:
+                best = (top, swaps, order)
+        top, swaps, order = best
+        for k in range(K):
+            gw[m * K + k][h] = k ^ ((swaps >> (k // 2)) & 1)
+            gw[c * K + k][h] = k ^ ((swaps >> (4 + k // 2)) & 1)
+        for i, q in enumerate(order):
+            gw[d * K + last[i][1]][h] = q
+    src = [dict() for r in range(n)]
+    for s in range(n):
+        for host, kg in gw[s].items():
+            src[host * K + kg][s // K] = s
+    plan["gw"], plan["src"] = gw, src
 
 
 def rank_program(g, core, T, topo):
@@ -95,21 +290,27 @@ def rank_program(g, core, T, topo):
     P = _CACHE["plan"]
     sem = T.sem
     h, k = rank // K, rank % K
-    rm_, rc_, rd_ = mate_host(h) * K + k, cable_host(h) * K + k, diag_host(h) * K + k
-    core_m, core_c = T.cores[rm_], T.cores[rc_]
+    hm, hc, hd = mate_host(h), cable_host(h), diag_host(h)
+    src_m, src_c, src_d = P["src"][rank][hm], P["src"][rank][hc], P["src"][rank][hd]
     queues = [g.sync, g.scalar]
     turn = [0]
     sent = [0]
+
+    def gateway(s, host):
+        return T.cores[host * K + P["gw"][s][host]]
 
     def both_wait(s, v):
         for q in queues:
             q.wait_ge(s, v)
 
-    def copy(out, in_, s):
-        q = queues[turn[0]]
-        turn[0] ^= 1
-        q.dma_start(out, in_).then_inc(s, 16)
-        return 16
+    def copy_runs(buf, j, pairs, s):
+        n = 0
+        for b, p, ln in runs(pairs):
+            queues[turn[0]].dma_start(buf[:, j:j + ln], T[b][:, p:p + ln]).then_inc(s, 16)
+            turn[0] ^= 1
+            j += ln
+            n += 16
+        return n
 
     def write(dst_core, out, in_, rsem):
         rid, pid = topo.addr(dst_core, core)
@@ -120,93 +321,61 @@ def rank_program(g, core, T, topo):
     g.sync.dma_start(T.xs[:], T.x[:]).then_inc(sem.ld, 16)
     both_wait(sem.ld, 16)
 
-    def pack(buf, order, s):
-        n, j = 0, 0
-        for b, p, ln in runs([("xs", t) for t in order]):
-            n += copy(buf[:, j:j + ln], T.xs[:, p:p + ln], s)
-            j += ln
-        return n
-
     cb, sw = P["cb"][rank], P["sw"][rank]
     assert len(cb) <= W_CB and len(sw) <= W_SW
-    n_pkc = pack(T.pcb, cb, sem.pkc)
-    n_pks = pack(T.psw, sw, sem.pks)
+    n_pkc = copy_runs(T.pcb, 0, [("xs", t) for t in cb], sem.pkc)
+    n_pks = copy_runs(T.psw, 0, [("xs", t) for t in sw], sem.pks)
 
     if cb:
         g.wait_ge(sem.pkc, n_pkc)
-        write(core_c, T.rc[:, 0:len(cb)], T.pcb[:, 0:len(cb)], sem.arrc)
+        write(gateway(rank, hc), T.rc[:, 0:len(cb)], T.pcb[:, 0:len(cb)], sem.arrc)
     if sw:
         g.wait_ge(sem.pks, n_pks)
-        write(core_m, T.rm[:, 0:len(sw)], T.psw[:, 0:len(sw)], sem.arrm)
+        write(gateway(rank, hm), T.rm[:, 0:len(sw)], T.psw[:, 0:len(sw)], sem.arrm)
 
-    in_c, in_cf = len(P["cb"][rc_]), P["cbf"][rc_]
-    in_m, in_mf = len(P["sw"][rm_]), P["swf"][rm_]
-    in_ds = len(P["cb"][rd_]) - P["cbf"][rd_]
-    in_dc = len(P["sw"][rd_]) - P["swf"][rd_]
+    in_c, in_cf = len(P["cb"][src_c]), P["cbf"][src_c]
+    in_m, in_mf = len(P["sw"][src_m]), P["swf"][src_m]
+    in_ds = len(P["cb"][src_d]) - P["cbf"][src_d]
+    in_dc = len(P["sw"][src_d]) - P["swf"][src_d]
     assert in_ds <= W_DS and in_dc <= W_DC
-    off_chip = popcount(topo.mask(core, core_c))
+    off_chip = popcount(topo.mask(core, T.cores[hc * K]))
 
     if in_c:
         g.wait_ge(sem.arrc, off_chip)
         if in_c > in_cf:
-            write(core_m, T.rds[:, 0:in_c - in_cf], T.rc[:, in_cf:in_c], sem.arrds)
+            write(gateway(src_c, hm), T.rds[:, 0:in_c - in_cf], T.rc[:, in_cf:in_c], sem.arrds)
     if in_m:
         g.wait_ge(sem.arrm, off_chip)
         if in_m > in_mf:
-            write(core_c, T.rdc[:, 0:in_m - in_mf], T.rm[:, in_mf:in_m], sem.arrdc)
+            write(gateway(src_m, hc), T.rdc[:, 0:in_m - in_mf], T.rm[:, in_mf:in_m], sem.arrdc)
 
-    def where(s, t):
-        if s == rank:
-            return ("xs", t)
-        if s == rm_:
-            return ("rm", P["swpos"][s][t])
-        if s == rc_:
-            return ("rc", P["cbpos"][s][t])
-        p = P["cbpos"][s].get(t, -1)
-        if p >= P["cbf"][s]:
-            return ("rds", p - P["cbf"][s])
-        return ("rdc", P["swpos"][s][t] - P["swf"][s])
-
-    st_col = [0]
-    groups = [(rank, sem.ga0, []), (rm_, sem.ga1, [(sem.arrm, in_m)]), (rc_, sem.ga2, [(sem.arrc, in_c)]),
-              (rd_, sem.ga3, [(sem.arrds, in_ds), (sem.arrdc, in_dc)])]
+    st_col = 0
+    groups = [(rank, sem.ga0, []), (src_m, sem.ga1, [(sem.arrm, in_m)]), (src_c, sem.ga2, [(sem.arrc, in_c)]),
+              (src_d, sem.ga3, [(sem.arrds, in_ds), (sem.arrdc, in_dc)])]
     deliveries = []
     for s, gsem, needs in groups:
         for a, width in needs:
             if width:
                 both_wait(a, off_chip)
-        n = 0
-        pieces = []
-        for e in range(h * K, h * K + K):
-            toks = P["toks"][s][e]
-            if not toks:
-                continue
-            if e == rank:
-                buf, j = T.ybuf, P["off"][s][e]
-            else:
-                buf, j = T.stage, st_col[0]
-                pieces.append((e, j, len(toks)))
-                st_col[0] += len(toks)
-            for b, p, ln in runs([where(s, t) for t in toks]):
-                n += copy(buf[:, j:j + ln], T[b][:, p:p + ln], gsem)
-                j += ln
-        deliveries.append((s, gsem, n, pieces))
-    assert st_col[0] <= W_ST
-    for s, gsem, n, pieces in deliveries:
+        staged, pieces, own = gather_of(P, s, h, k)
+        n = copy_runs(T.stage, st_col, staged, gsem)
+        n += copy_runs(T.ybuf, P["off"][s][rank], own, gsem)
+        deliveries.append((s, gsem, n, st_col, pieces))
+        st_col += len(staged)
+    assert st_col <= W_ST
+
+    for s, gsem, n, base, pieces in deliveries:
         if n:
             g.wait_ge(gsem, n)
         for e, j, ln in pieces:
             o = P["off"][s][e]
-            write(T.cores[e], T.ybuf[:, o:o + ln], T.stage[:, j:j + ln], sem.arrp)
+            write(T.cores[e], T.ybuf[:, o:o + ln], T.stage[:, base + j:base + j + ln], sem.arrp)
 
     n_in = 0
-    for gw in range(h * K, h * K + K):
-        if gw == rank:
-            continue
-        kk = gw % K
-        for hh in range(HOSTS):
-            if P["toks"][hh * K + kk][rank]:
-                n_in += popcount(topo.mask(T.cores[gw], core))
+    for s in range(len(P["gw"])):
+        kg = P["gw"][s][h]
+        if kg != k and P["toks"][s][rank]:
+            n_in += popcount(topo.mask(T.cores[h * K + kg], core))
     if n_in:
         g.wait_ge(sem.arrp, n_in)
     tot = P["tot"][rank]

@@ -3,7 +3,7 @@ import numpy as np
 K = 8
 HOSTS = 4
 
-W_CB, W_SW, W_DS, W_DC, W_ST, W_Y = 128, 128, 128, 128, 512, 549
+W_CB, W_SW, W_DS, W_DC, W_ST, W_Y = 102, 101, 73, 34, 473, 549
 SCRATCH = {
     "xs": ("sbuf", [128, 128], "float32"),
     "pcb": ("sbuf", [128, W_CB], "float32"),

import numpy as np

K = 8
HOSTS = 4

W_CB, W_SW, W_DS, W_DC, W_ST, W_Y = 102, 101, 73, 34, 473, 549
SCRATCH = {
    "xs": ("sbuf", [128, 128], "float32"),
    "pcb": ("sbuf", [128, W_CB], "float32"),
    "psw": ("sbuf", [128, W_SW], "float32"),
    "rc": ("sbuf", [128, W_CB], "float32"),
    "rm": ("sbuf", [128, W_SW], "float32"),
    "rds": ("sbuf", [128, W_DS], "float32"),
    "rdc": ("sbuf", [128, W_DC], "float32"),
    "stage": ("sbuf", [128, W_ST], "float32"),
    "ybuf": ("sbuf", [128, W_Y], "float32"),
}
SEMAPHORES = ["ld", "pkc", "pks", "arrc", "arrm", "arrds", "arrdc", "ga0", "ga1", "ga2", "ga3", "arrp", "sent", "st"]

_CACHE = {}


def mate_host(h):
    return h ^ 1


def cable_host(h):
    return 3 - h


def diag_host(h):
    return (h + 2) % 4


def popcount(x):
    return bin(x).count("1")


def runs(pairs):
    out = []
    for b, p in pairs:
        if out and out[-1][0] == b and out[-1][1] + out[-1][2] == p:
            out[-1][2] += 1
        else:
            out.append([b, p, 1])
    return out


def assign_max(w):
    n = w.shape[0]
    cost = (w.max() - w).astype(np.float64)
    big = 1e18
    u, v = np.zeros(n + 1), np.zeros(n + 1)
    p, way = np.zeros(n + 1, dtype=np.int64), np.zeros(n + 1, dtype=np.int64)
    for i in range(1, n + 1):
        p[0] = i
        j0 = 0
        minv = np.full(n + 1, big)
        used = np.zeros(n + 1, dtype=bool)
        while True:
            used[j0] = True
            i0 = p[j0]
            cur = cost[i0 - 1] - u[i0] - v[1:]
            free = ~used[1:]
            better = free & (cur < minv[1:])
            minv[1:][better] = cur[better]
            way[1:][better] = j0
            cand = np.where(free, minv[1:], big)
            j1 = int(np.argmin(cand)) + 1
            delta = cand[j1 - 1]
            u[p[used]] += delta
            v[used] -= delta
            minv[1:][free] -= delta
            j0 = j1
            if p[j0] == 0:
                break
        while j0 != 0:
            j1 = way[j0]
            p[j0] = p[j1]
            j0 = j1
    col = [0] * n
    for j in range(1, n + 1):
        col[p[j] - 1] = j - 1
    return col


def chain(seg, lists):
    n = len(seg)
    if n < 2:
        return list(seg)
    idx = dict((t, i) for i, t in enumerate(seg))
    w = np.zeros((n, n))
    for t in seg:
        if t + 1 in idx:
            w[idx[t], idx[t + 1]] += 1
    for lst in lists:
        for a, b in zip(lst, lst[1:]):
            if a in idx and b in idx and a < b:
                w[idx[a], idx[b]] += 1
    col = assign_max(w)
    nxt, has_pred = {}, set()
    for i in range(n):
        if w[i, col[i]] > 0:
            nxt[seg[i]] = seg[col[i]]
            has_pred.add(seg[col[i]])
    out = []
    for t in seg:
        if t not in has_pred:
            out.append(t)
            while out[-1] in nxt:
                out.append(nxt[out[-1]])
    return out


def links_of(s, via_c):
    h, k = s // K, s % K
    if via_c:
        return (h, k // 2), (cable_host(h), k // 4)
    return (mate_host(h), k // 2), (h, k // 4)


def make_plan(route, ntok):
    n = len(route)
    toks = [[[] for e in range(n)] for s in range(n)]
    for s in range(n):
        for t in range(ntok):
            for e in route[s][t]:
                toks[s][e].append(t)
    off = [[0] * n for s in range(n)]
    tot = [0] * n
    for e in range(n):
        for s in range(n):
            off[s][e] = tot[e]
            tot[e] += len(toks[s][e])

    segs = [dict((x, []) for x in ("ca", "cb", "cc", "ma", "mb", "mc")) for s in range(n)]
    cable = dict(((h, p), 0) for h in range(HOSTS) for p in range(K // 2))
    port = dict(((h, q), 0) for h in range(HOSTS) for q in range(2))
    loose = []
    for s in range(n):
        h, k = s // K, s % K
        m, c, d = mate_host(h), cable_host(h), diag_host(h)
        for t in range(ntok):
            hs = set(e // K for e in route[s][t])
            if c in hs:
                segs[s]["cb" if d in hs else "ca"].append(t)
                cable[(h, k // 2)] += 1
                if d in hs:
                    port[(c, k // 4)] += 1
                if m in hs:
                    segs[s]["ma"].append(t)
                    port[(h, k // 4)] += 1
            elif m in hs:
                segs[s]["mb" if d in hs else "ma"].append(t)
                port[(h, k // 4)] += 1
                if d in hs:
                    cable[(m, k // 2)] += 1
            elif d in hs:
                loose.append((s, t))

    mean_c = (sum(cable.values()) + len(loose)) / float(len(cable))
    mean_p = (sum(port.values()) + len(loose)) / float(len(port))

    def price(s, via_c):
        a, b = links_of(s, via_c)
        return (((cable[a] + 1) / mean_c) ** 8 - (cable[a] / mean_c) ** 8
                + ((port[b] + 1) / mean_p) ** 8 - (port[b] / mean_p) ** 8)

    def load(s, via_c, x):
        a, b = links_of(s, via_c)
        cable[a] += x
        port[b] += x

    way = {}
    for s, t in loose:
        way[(s, t)] = price(s, True) <= price(s, False)
        load(s, way[(s, t)], 1)
    for sweep in range(20):
        moved = False
        for s, t in loose:
            v = way[(s, t)]
            load(s, v, -1)
            if price(s, not v) < price(s, v) - 1e-12:
                v = not v
                moved = True
            way[(s, t)] = v
            load(s, v, 1)
        if not moved:
            break
    for s, t in loose:
        segs[s]["cc" if way[(s, t)] else "mc"].append(t)

    plan = {"toks": toks, "off": off, "tot": tot, "cb": [], "sw": [], "cbf": [], "swf": [], "cbpos": [], "swpos": [],
            "cable": cable, "port": port}
    for s in range(n):
        h = s // K
        m, c, d = mate_host(h), cable_host(h), diag_host(h)

        def lists(hosts):
            return [toks[s][e] for e in range(n) if e // K in hosts]

        sg = segs[s]
        cb = chain(sg["ca"], lists([c])) + chain(sg["cb"], lists([c, d])) + chain(sg["cc"], lists([d]))
        sw = chain(sg["ma"], lists([m])) + chain(sg["mb"], lists([m, d])) + chain(sg["mc"], lists([d]))
        plan["cb"].append(cb)
        plan["sw"].append(sw)
        plan["cbf"].append(len(sg["ca"]))
        plan["swf"].append(len(sg["ma"]))
        plan["cbpos"].append(dict((t, i) for i, t in enumerate(cb)))
        plan["swpos"].append(dict((t, i) for i, t in enumerate(sw)))
    choose_gateways(plan, n)
    return plan


def where(plan, s, host, t):
    h = s // K
    if host == h:
        return ("xs", t)
    if host == mate_host(h):
        return ("rm", plan["swpos"][s][t])
    if host == cable_host(h):
        return ("rc", plan["cbpos"][s][t])
    p = plan["cbpos"][s].get(t, -1)
    if p >= plan["cbf"][s]:
        return ("rds", p - plan["cbf"][s])
    return ("rdc", plan["swpos"][s][t] - plan["swf"][s])


def gather_of(plan, s, host, kg):
    staged, pieces, own = [], [], []
    for e in range(host * K, host * K + K):
        cols = [where(plan, s, host, t) for t in plan["toks"][s][e]]
        if e == host * K + kg:
            own = cols
        elif cols:
            pieces.append((e, len(staged), len(cols)))
            staged += cols
    return staged, pieces, own


def choose_gateways(plan, n):
    memo = {}

    def cost(s, host, kg):
        if (s, host, kg) not in memo:
            staged, pieces, own = gather_of(plan, s, host, kg)
            memo[(s, host, kg)] = len(runs(staged)) + len(runs(own))
        return memo[(s, host, kg)]

    gw = [dict() for s in range(n)]
    for h in range(HOSTS):
        m, c, d = mate_host(h), cable_host(h), diag_host(h)
        fixed = []
        for k in range(K):
            s = h * K + k
            gw[s][h] = k
            fixed.append(len(runs([("xs", t) for t in plan["cb"][s]])) + len(runs([("xs", t) for t in plan["sw"][s]]))
                         + cost(s, h, k))
        last = sorted(((cost(d * K + k, h, k), k) for k in range(K)), reverse=True)
        best = None
        for swaps in range(1 << K):
            work = list(fixed)
            for k in range(K):
                km, kc = k ^ ((swaps >> (k // 2)) & 1), k ^ ((swaps >> (4 + k // 2)) & 1)
                work[km] += cost(m * K + k, h, km)
                work[kc] += cost(c * K + k, h, kc)
            order = sorted(range(K), key=lambda q: work[q])
            top = max(work[q] + last[i][0] for i, q in enumerate(order))
            if best is None or top < best[0]:
                best = (top, swaps, order)
        top, swaps, order = best
        for k in range(K):
            gw[m * K + k][h] = k ^ ((swaps >> (k // 2)) & 1)
            gw[c * K + k][h] = k ^ ((swaps >> (4 + k // 2)) & 1)
        for i, q in enumerate(order):
            gw[d * K + last[i][1]][h] = q
    src = [dict() for r in range(n)]
    for s in range(n):
        for host, kg in gw[s].items():
            src[host * K + kg][s // K] = s
    plan["gw"], plan["src"] = gw, src


def rank_program(g, core, T, topo):
    rank = T.rank_of(core)
    if rank is None:
        return
    if "plan" not in _CACHE:
        _CACHE["plan"] = make_plan(T.tables["ROUTE"], T.tables["T"])
    P = _CACHE["plan"]
    sem = T.sem
    h, k = rank // K, rank % K
    hm, hc, hd = mate_host(h), cable_host(h), diag_host(h)
    src_m, src_c, src_d = P["src"][rank][hm], P["src"][rank][hc], P["src"][rank][hd]
    queues = [g.sync, g.scalar]
    turn = [0]
    sent = [0]

    def gateway(s, host):
        return T.cores[host * K + P["gw"][s][host]]

    def both_wait(s, v):
        for q in queues:
            q.wait_ge(s, v)

    def copy_runs(buf, j, pairs, s):
        n = 0
        for b, p, ln in runs(pairs):
            queues[turn[0]].dma_start(buf[:, j:j + ln], T[b][:, p:p + ln]).then_inc(s, 16)
            turn[0] ^= 1
            j += ln
            n += 16
        return n

    def write(dst_core, out, in_, rsem):
        rid, pid = topo.addr(dst_core, core)
        mask = topo.mask(core, dst_core)
        g.remote_dma(out, in_, rsem, sem.sent, pid, rid, mask)
        sent[0] += popcount(mask)

    g.sync.dma_start(T.xs[:], T.x[:]).then_inc(sem.ld, 16)
    both_wait(sem.ld, 16)

    cb, sw = P["cb"][rank], P["sw"][rank]
    assert len(cb) <= W_CB and len(sw) <= W_SW
    n_pkc = copy_runs(T.pcb, 0, [("xs", t) for t in cb], sem.pkc)
    n_pks = copy_runs(T.psw, 0, [("xs", t) for t in sw], sem.pks)

    if cb:
        g.wait_ge(sem.pkc, n_pkc)
        write(gateway(rank, hc), T.rc[:, 0:len(cb)], T.pcb[:, 0:len(cb)], sem.arrc)
    if sw:
        g.wait_ge(sem.pks, n_pks)
        write(gateway(rank, hm), T.rm[:, 0:len(sw)], T.psw[:, 0:len(sw)], sem.arrm)

    in_c, in_cf = len(P["cb"][src_c]), P["cbf"][src_c]
    in_m, in_mf = len(P["sw"][src_m]), P["swf"][src_m]
    in_ds = len(P["cb"][src_d]) - P["cbf"][src_d]
    in_dc = len(P["sw"][src_d]) - P["swf"][src_d]
    assert in_ds <= W_DS and in_dc <= W_DC
    off_chip = popcount(topo.mask(core, T.cores[hc * K]))

    if in_c:
        g.wait_ge(sem.arrc, off_chip)
        if in_c > in_cf:
            write(gateway(src_c, hm), T.rds[:, 0:in_c - in_cf], T.rc[:, in_cf:in_c], sem.arrds)
    if in_m:
        g.wait_ge(sem.arrm, off_chip)
        if in_m > in_mf:
            write(gateway(src_m, hc), T.rdc[:, 0:in_m - in_mf], T.rm[:, in_mf:in_m], sem.arrdc)

    st_col = 0
    groups = [(rank, sem.ga0, []), (src_m, sem.ga1, [(sem.arrm, in_m)]), (src_c, sem.ga2, [(sem.arrc, in_c)]),
              (src_d, sem.ga3, [(sem.arrds, in_ds), (sem.arrdc, in_dc)])]
    deliveries = []
    for s, gsem, needs in groups:
        for a, width in needs:
            if width:
                both_wait(a, off_chip)
        staged, pieces, own = gather_of(P, s, h, k)
        n = copy_runs(T.stage, st_col, staged, gsem)
        n += copy_runs(T.ybuf, P["off"][s][rank], own, gsem)
        deliveries.append((s, gsem, n, st_col, pieces))
        st_col += len(staged)
    assert st_col <= W_ST

    for s, gsem, n, base, pieces in deliveries:
        if n:
            g.wait_ge(gsem, n)
        for e, j, ln in pieces:
            o = P["off"][s][e]
            write(T.cores[e], T.ybuf[:, o:o + ln], T.stage[:, base + j:base + j + ln], sem.arrp)

    n_in = 0
    for s in range(len(P["gw"])):
        kg = P["gw"][s][h]
        if kg != k and P["toks"][s][rank]:
            n_in += popcount(topo.mask(T.cores[h * K + kg], core))
    if n_in:
        g.wait_ge(sem.arrp, n_in)
    tot = P["tot"][rank]
    assert tot <= W_Y
    g.dma_start(T.y[:, 0:tot], T.ybuf[:, 0:tot]).then_inc(sem.st, 16)
    g.wait_ge(sem.st, 16)
    g.wait_ge(sem.sent, sent[0])
